import numpy as np, ml_dtypes
CORES = [23,119,17,113]
N = 4
import mx_ref
BF = ml_dtypes.bfloat16
def pick(q, e):
    c = np.concatenate([q[0].reshape(128, -1, 4), np.zeros((128, 1, 4), np.uint8)], axis=1); s = np.concatenate([q[1], np.ones((16, 1), np.uint8)], axis=1)
    return (np.ascontiguousarray(c[:, e].reshape(128, -1)), np.ascontiguousarray(s[:, e]))
def join(*qs):
    return (np.concatenate([q[0] for q in qs], axis=1), np.concatenate([q[1] for q in qs], axis=1))
def put(q, e, v):
    c, s = q[0].reshape(128, -1, 4).copy(), q[1].copy(); c[:, e] = v[0].reshape(128, -1, 4); s[:, e] = v[1]
    return (c.reshape(128, -1), s)
def pk(c, s):
    return (np.ascontiguousarray(c), mx_ref.live(s))
def emit(q):
    return q[0], q[1]
def tile(rs):
    return np.stack(rs, axis=2).reshape(128, -1).astype(BF)
def cut(t, i, w=512):
    return t[:, w * i:w * i + w]
def f(rng, *shape):
    return mx_ref.flush((rng.standard_normal(shape, dtype=np.float32) * np.exp2(rng.integers(-2, 3, shape[:-1] + (1,)))).astype(BF))
def wide(rng, *shape, cols=0):
    v = rng.standard_normal(shape, dtype=np.float32) * np.exp2(rng.integers(-12, 13, shape)).astype(np.float32)
    if cols: v *= np.repeat(np.exp2(rng.integers(-cols, cols + 1, shape[:-2] + (1, shape[-1] // 4))) * (rng.random(shape[:-2] + (1, shape[-1] // 4)) > 0.0625), 4, axis=-1).astype(np.float32)
    return mx_ref.flush(v.astype(BF))
P, CAPP, L, CB = 256, 128, 2, 128
def big(v, k):
    v = v.astype(np.float32) * np.float32(k)
    v[np.abs(v) < np.float32(2.0 ** -10)] = 0
    return v.astype(BF)
def number(z):
    n = np.zeros(z.shape[1], np.int64)
    for b in range(L): n += (z[b] < 0) * (1 << b)
    return n
def buckets(x, pl):
    X = [mx_ref.quantize(np.ascontiguousarray(x[s])) for s in range(N)]
    return X, np.stack([number(mx_ref.matmul(mx_ref.quantize(np.ascontiguousarray(pl[s])), X[s])) for s in range(N)])
def taken(bk):
    at = np.full((N, N, CAPP), -1)
    for d in range(N):
        for s in range(N):
            e = np.flatnonzero(bk[s] == d)[:CAPP]
            at[d, s, :e.size] = e
    return at
def attend(c, wv, e):
    e = np.concatenate([e, np.setdiff1d(np.arange(512), e)[:max(4 - len(e), len(e) % 2)]])
    m = pick(c, e)
    ct = [pick(c, np.arange(t, 512, 4)) for t in range(4)]
    A = tile([np.float32(0.0625) * np.maximum(mx_ref.matmul(k, m) + np.float32(0), np.float32(0)) for k in ct])
    qw = mx_ref.quantize(np.ascontiguousarray(wv))
    V = tile([mx_ref.matmul(k, qw) for k in ct])
    qa = mx_ref.quantize(A)
    O = [mx_ref.matmul(mx_ref.quantize(np.ascontiguousarray(cut(V, i))), qa) for i in range(4)]
    h = np.zeros((128, 512, 4), BF)
    h[:, e] = tile([np.float32(0.0625) * o for o in O]).reshape(128, -1, 4)
    return A, V, h.reshape(128, 2048)
def planes(rng):
    p = np.array(f(rng, 128, 512))
    p[:, 4 * L:] = 0
    return np.stack([p] * N)
def plain(rng):
    return {"x": big(f(rng, N, 128, 4 * P), 0.25), "pl": planes(rng), "p2": planes(rng), "wv": big(f(rng, N, 128, 2048), 0.25), "w": f(rng, N, 128, 512)}
def aimed(rng, d, want, gone=0, then=None, two=None):
    x, p = d["x"].astype(np.float32).reshape(N, 128, P, 4), np.zeros((128, 128, 4), np.float32)
    gone = np.zeros((N, P), np.int64) + gone
    at = rng.permutation(128)[:16 * L + 16].reshape(L + 1, 16)
    side = np.zeros((N, 128, 4), np.float32)
    for b in range(L):
        v = (1 + rng.random((16, 4))) * rng.choice([-1.0, 1.0], (16, 4))
        p[at[b], b] = v
        turn = (1 - 2 * (want >> b & 1)) * (1 - (gone >> b & 1))
        x[:, at[b]] = np.abs(x[:, at[b]]) * (np.sign(v)[None, :, None, :] * turn[:, None, :, None]) * (0.0625 if then is None else 1.0)
        side[:, at[b]] = np.sign(v)[None] * (1 - 2 * (np.arange(N) >> b & 1))[:, None, None]
    parted = np.zeros((128, 4), np.float32)
    if two is not None:
        k = two[2][:, None, :, None]
        u = rng.choice([-1.0, 1.0], (16, 4))
        parted[at[L]] = u
        x = np.where(k != 0, np.float32(0.125) * x, x)
        x[:, at[L]] = np.where(k != 0, 0.5 * (1 + rng.random((N, 16, P, 4))) * u[None, :, None, :] * k, x[:, at[L]])
    x = x * (gone != N - 1)[:, None, :, None]
    d = {**d, "x": big(x.reshape(N, 128, 4 * P), 1), "pl": np.stack([p.reshape(128, 512).astype(BF)] * N)}
    if then is None: return d
    p2, wv = np.zeros((128, 128, 4), np.float32), d["wv"].astype(np.float32).reshape(N, 128, 4, 128, 4)
    on = rng.permutation(128)[:16 * L].reshape(L, 16)
    for b in range(L):
        p2[on[b], b] = 1 + rng.random((16, 4))
        for q in range(N):
            sign = parted if two is not None and q == two[0] and b == two[1] else side[q]
            wv[q][:, :, on[b]] = np.abs(wv[q][:, :, on[b]]) * sign[:, None, None, :] * (1 - 2 * (int(then[q]) >> b & 1))
    return {**d, "wv": big(wv.reshape(N, 128, 2048), 1), "p2": np.stack([p2.reshape(128, 512).astype(BF)] * N)}
def setup_inputs(rng):
    return plain(rng)
def setup_inputs_crowd(rng):
    h, g = (int(v) for v in rng.permutation(N)[:2])
    c, then = rng.permutation(N), np.zeros(N, np.int64)
    then[c] = np.roll(c, 1)
    bit = int(rng.choice([b for b in range(L) if int(then[h]) ^ (1 << b) != h]))
    one = int(rng.choice([q for q in range(N) if q not in (h, g) and int(then[q]) != int(then[h]) ^ (1 << bit)]))
    others = np.delete(np.arange(N), [h, g, one])
    o, n = rng.permutation(N), np.full(N, CAPP)
    n[o[N // 2:]] += rng.integers(1, P - CAPP + 1, N - N // 2)
    n[o[-1]] = P
    r, more = int(o[N // 2]), P // (CAPP + 1) - 1
    if more: n[r] = rng.integers(CAPP + 1, P - more * (CAPP + 1) + 1)
    want = rng.choice(others, (N, P))
    for s in range(N): want[s, rng.permutation(P)[:n[s]]] = h
    e = rng.permutation(np.flatnonzero((want != h) & (np.arange(N) != r)[:, None]))
    want.flat[e[:CB]] = g
    want.flat[e[CB]] = one
    if more:
        e = rng.permutation(np.flatnonzero(want[r] != h))
        want[r, e[:more * (CAPP + 1)]] = np.repeat(rng.choice(others, more, replace=False), CAPP + 1)
    kind = np.zeros((N, P), np.int64)
    for s in range(N):
        e = np.flatnonzero(want[s] == h)
        kind[s, e] = 1 - 2 * ((np.arange(e.size) + int(rng.integers(0, 2))) % 2)
    return aimed(rng, plain(rng), want, then=then, two=(h, bit, kind))
def setup_inputs_few(rng):
    o = rng.permutation(N)
    want = rng.choice(o[2:], (N, P))
    want[int(rng.integers(0, N)), int(rng.integers(0, P))] = o[0]
    return aimed(rng, plain(rng), want)
def setup_inputs_neg(rng):
    d, g = plain(rng), rng.permutation(16)
    want = np.stack([rng.permutation(P) % N for s in range(N)])
    part = 8 * g[:, None] + np.arange(8)
    rows = (4 * part[L:].reshape(-1)[:, None] + np.arange(4)).reshape(-1)
    x, p = np.zeros((N, P, 512)), np.zeros((128, 128, 4))
    for b in range(L):
        v = rng.choice([-1.0, 1.0], (8, 4))
        p[part[b], b] = v * (1 + rng.random((8, 4)))
        e = (4 * part[b][:, None] + np.arange(4)).reshape(-1)
        x[:, :, e] = 2.0 ** -8 * v.reshape(-1) * (1 - 2 * (want >> b & 1))[:, :, None]
    for q in range(N):
        s, i = np.nonzero(want == q)
        v = np.full((P, P), -2.0 ** -7)
        v[np.arange(P), np.arange(P)] = P * 2.0 ** -7
        x[s[:, None], i[:, None], rng.permutation(rows)[:P][None, :]] = v * rng.choice([-1.0, 1.0], P)
    x *= np.exp2(rng.integers(-1, 2, (N, P, 1)))
    x = np.ascontiguousarray(x.reshape(N, P, 128, 4).transpose(0, 2, 1, 3)).reshape(N, 128, 4 * P)
    return {**d, "x": x.astype(np.float32).astype(BF), "pl": np.stack([p.reshape(128, 512).astype(np.float32).astype(BF)] * N)}
def setup_inputs_zero(rng):
    gone = np.zeros((N, P), np.int64)
    for s in range(N):
        e = rng.permutation(P)
        gone[s, e[:P // 4]] = N - 1
        gone[s, e[P // 4:P // 2]] = 1 << rng.integers(0, L, P // 2 - P // 4)
    d = aimed(rng, plain(rng), rng.integers(0, N, (N, P)), gone)
    b, q, on = int(rng.integers(0, L)), int(rng.integers(0, N)), rng.permutation(128)[:16]
    p2, wv = np.array(d["p2"]).reshape(N, 128, 128, 4), np.array(d["wv"]).reshape(N, 128, 4, 128, 4)
    p2[:, np.setdiff1d(np.arange(128), on), b] = 0
    wv[q][:, :, on] = 0
    return {**d, "p2": p2.reshape(N, 128, 512), "wv": wv.reshape(N, 128, 2048)}
def setup_inputs_spread(rng):
    return {**plain(rng), "x": big(wide(rng, N, 128, 4 * P, cols=2), 2.0 ** -10)}
def check_inputs(d):
    b = []
    for k in ("x", "pl", "p2", "wv", "w"):
        v = np.abs(d[k].astype(np.float32))
        if not (np.isfinite(v).all() and ((v == 0) | (v >= 2.0 ** -30) & (v <= 2.0 ** 30)).all()): b.append("a value of " + k)
    for k in ("pl", "p2"):
        p = d[k].astype(np.float32)
        if (p[:, :, 4 * L:] != 0).any(): b.append(k + " has numbers behind its first L columns")
        if (p != p[:1]).any(): b.append(k + " isn't the same on all ranks")
    return b
def reference(x, pl, p2, wv, w):
    X, bk = buckets(x, pl)
    at = taken(bk)
    H, num, to = [], [], []
    for d in range(N):
        c = join(*[pick(X[s], at[d, s]) for s in range(N)])
        A, V, h = attend(c, wv[d], np.flatnonzero(at[d].reshape(-1) >= 0))
        h = mx_ref.quantize(h)
        n = np.concatenate([np.where(at[d, s] >= 0, P * s + at[d, s], -1) for s in range(N)])
        H.append(h)
        num.append(n)
        to.append(np.where(n >= 0, number(mx_ref.matmul(mx_ref.quantize(np.ascontiguousarray(p2[d])), h)), -1))
    H = join(*H)
    num = np.concatenate(num + [np.full(1, -1)])
    oc, osc = np.zeros((N, 128, 4 * N * CB), np.uint8), np.zeros((N, 16, N * CB), np.uint8)
    nb, y = np.zeros((N, 1, N * CB), np.float32), np.zeros((N, 128, N * CB), np.float32)
    for e in range(N):
        k = np.full(N * CB, -1)
        for d in range(N):
            i = np.flatnonzero(to[d] == e)[:CB]
            k[d * CB + np.arange(i.size)] = 512 * d + i
        h = pick(H, k)
        oc[e], osc[e] = emit(h)
        nb[e, 0] = num[k]
        y[e] = mx_ref.matmul(mx_ref.quantize(np.ascontiguousarray(w[e])), h)
    return {"oc": oc, "osc": osc, "id": nb, "y": y}

@@ -1,0 +1,444 @@
+from concourse.bass import DstId, RemoteDMATransfer
+from concourse.mybir import dt, AluOpType, AxisListType, ActivationFunctionType
+
+F, B, I, U = "float32", "bfloat16", "int32", "uint16"
+Q, S8 = "float8_e4m3fn_x4", "uint8"
+COL = {n: ("ki", k) for k, n in enumerate(("pc", "b3", "b4", "bb", "qi", "gi", "oi", "ji"))}
+COL.update({n: ("kf", k) for k, n in enumerate((
+    "thr", "bd", "bias", "init1", "h16", "q4", "qf", "gf", "oddf", "evf", "t15", "hc", "t512", "j0", "init2", "cnt2"))})
+SCRATCH = {}
+for _n, _w, _t in (
+        ("plb", 8, B), ("p2b", 8, B), ("xb", 1024, B), ("wvb", 2048, B), ("wb", 512, B),
+        ("w1t", 1024, B), ("zt", 512, B), ("w2t", 1088, B), ("at", 2048, B), ("vt", 2048, B), ("ht", 2048, B),
+        ("sg0", 20, B), ("sg1", 20, B), ("val1", 128, B), ("val2", 256, B), ("win1", 1024, B), ("win2", 2432, B),
+        ("ki", 8, I), ("kf", 16, F),
+        ("vb1", 128, F), ("ctb", 32, F), ("ctf", 32, F), ("j8", 128, F), ("d0", 128, F), ("plc", 256, F), ("pib", 256, F),
+        ("va", 256, F), ("vp", 256, F), ("c8", 32, F), ("dm1", 32, F), ("q16", 64, F), ("dm2", 64, F), ("io2", 128, F),
+        ("nadd", 32, F), ("zf", 256, F), ("X", 32, F), ("xt", 32, F), ("fF", 32, F), ("nf", 32, F), ("nt", 32, F),
+        ("te", 128, F), ("thrm", 128, F), ("tabrow", 520, F), ("tab", 520, F),
+        ("u1", 256, F), ("mz1", 256, F), ("ind1", 256, F), ("C1", 256, F), ("M1", 256, F), ("df1", 8, F), ("l1", 32, F),
+        ("u2", 128, F), ("mz2", 128, F), ("ind2", 128, F), ("C2", 128, F), ("pen", 128, F), ("mb", 256, F), ("tt", 256, F),
+        ("base", 128, F), ("pd", 32, F), ("pdr", 4, F), ("ga", 64, F), ("gm", 64, F), ("idr", 4, F), ("idf", 4, F),
+        ("yb", 512, F),
+        ("do1", 8, U), ("do2", 16, U), ("off1", 32, U), ("off2", 32, U), ("offct", 32, U), ("offD", 4, U), ("nl", 32, U),
+        ("idu", 4, U), ("idl", 32, U)):
+    SCRATCH[_n] = ("sbuf", [128, _w], _t)
+for _n, _a, _b, _t in (("t13", 8, 32, F), ("u13", 8, 2, F), ("wd1", 32, 32, B), ("t21", 32, 32, B), ("D3", 4, 32, F),
+                       ("E3", 4, 16, F), ("F3", 4, 8, F), ("dst3", 4, 4, F), ("dumpc", 4, 4, F), ("wd2", 32, 32, B),
+                       ("t22", 32, 32, B), ("l2", 32, 2, F)):
+    SCRATCH[_n] = ("sbuf", [128, _a, _b], _t)
+for _n, _w in (("w1", 256), ("xq", 384), ("slota", 384), ("landa", 512), ("ct", 512), ("wvq", 512), ("aq", 512), ("vq", 512),
+               ("w2", 272), ("hq", 640), ("slotb", 384), ("landb", 512), ("wq", 128)):
+    SCRATCH[_n + "c"] = ("sbuf", [128, _w], Q)
+    SCRATCH[_n + "s"] = ("sbuf", [128, _w], S8)
+for _k in range(8):
+    SCRATCH["ps%d" % _k] = ("psum", [128, 512], F)
+
+SEMAPHORES = (["sv", "sa", "sp", "sg", "sent", "c1", "n1", "n2", "lpl", "lx0", "lx1", "lp2", "lwv", "lw", "ltb"]
+              + ["c2_%d" % k for k in range(4)] + ["%s%d" % (n, k) for n in ("oc", "os", "yy", "ii") for k in range(4)])
+
+TINY = 2.0 ** -120
+FAR = 8192.0
+LOW = -2.0 ** 99
+
+
+def rank_program(g, core, T, topo):
+    rank = T.rank_of(core)
+    if rank is None:
+        return
+    N = len(T.cores)
+    A, ACT = AluOpType, ActivationFunctionType
+    eng = {"v": g.vector, "a": g.scalar, "p": g.tensor, "g": g, "s": g.sync}
+    csem = {"v": "sv", "a": "sa", "p": "sp", "g": "sg"}
+    total, waited, know, acc = {}, {}, {q: {} for q in eng}, {}
+
+    def clash(x, y):
+        if x[1] >= y[2] or y[1] >= x[2]:
+            return False
+        if x[3] == y[3] and x[3] > 1:
+            a, b = x[1] % x[3], y[1] % y[3]
+            return a < b + y[4] and b < a + x[4]
+        return True
+
+    def order(q, tok):
+        sem, n, clock = tok
+        k = know[q]
+        if k.get(sem, 0) < n:
+            eng[q].wait_ge(T.sem[sem], n)
+            waited[sem] = max(waited.get(sem, 0), n)
+            k[sem] = n
+        for s, m in clock.items():
+            if k.get(s, 0) < m:
+                k[s] = m
+
+    def touch(q, reads, writes):
+        todo = []
+        for kind, specs in ((0, reads), (1, writes)):
+            for sp in specs:
+                for old, okind, tok, oq in acc.get(sp[0], ()):
+                    if sp[0][:2] == "ps":
+                        if oq != q:
+                            todo.append(tok)
+                    elif (kind or okind) and clash(sp, old):
+                        todo.append(tok)
+        todo.sort(key=lambda t: (t[0], -t[1]))
+        for t in todo:
+            order(q, t)
+
+    def note(q, tok, reads, writes):
+        for kind, specs in ((0, reads), (1, writes)):
+            for sp in specs:
+                acc.setdefault(sp[0], []).append((sp, kind, tok, q))
+
+    def v2(name, a, b, step=1):
+        return (T[name][:, a:b:step] if step > 1 else T[name][:, a:b], [(name, a, b, step, 1)], [])
+
+    def one(n):
+        return v2(COL[n][0], COL[n][1], COL[n][1] + 1)
+
+    def v3(name, a, b, c, d, step=1):
+        w = SCRATCH[name][1][2]
+        return (T[name][:, a:b, c:d:step] if step > 1 else T[name][:, a:b, c:d],
+                [(name, a * w + c, (b - 1) * w + d, w, d - c)], [])
+
+    def v3i(name, a, b, c):
+        w = SCRATCH[name][1][2]
+        return (T[name][:, a:b, c], [(name, a * w + c, (b - 1) * w + c + 1, w, 1)], [])
+
+    def codes(name, a, b, bits=None):
+        ap = T[name + "c"][:, a:b]
+        return (ap.bitcast(bits) if bits else ap, [(name + "c", a, b, 1, 1)], [])
+
+    def plane(name, a, b):
+        return v2(name + "s", a, b)
+
+    def by(win, off):
+        return (win[0].indirect(off[0]), win[1], off[1])
+
+    calls = {"tensor_copy": g.vector.tensor_copy, "tensor_tensor": g.vector.tensor_tensor, "memset": g.vector.memset,
+             "tensor_reduce": g.vector.tensor_reduce, "tensor_scalar": g.vector.tensor_scalar,
+             "tensor_tensor_scan": g.vector.tensor_tensor_scan, "transpose": g.vector.transpose,
+             "quantize_mx": g.vector.quantize_mx, "activation": g.scalar.activation, "matmul_mx": g.tensor.matmul_mx,
+             "iota": g.iota, "partition_broadcast": g.partition_broadcast}
+
+    def do(q, call, *args, outs=1, **kw):
+        reads, writes, plain = [], [], []
+        for i, x in enumerate(args):
+            if isinstance(x, tuple):
+                (writes if i < outs else reads).extend(x[1])
+                reads.extend(x[2])
+                plain.append(x[0])
+            else:
+                plain.append(x)
+        for k in kw:
+            if isinstance(kw[k], tuple):
+                reads.extend(kw[k][1])
+                kw[k] = kw[k][0]
+        touch(q, reads, writes)
+        s = csem[q]
+        calls[call](*plain, **kw).then_inc(T.sem[s], 1)
+        total[s] = total.get(s, 0) + 1
+        note(q, (s, total[s], dict(know[q])), reads, writes)
+
+    def dma(q, sem, out, in_):
+        touch(q, in_[1], out[1])
+        eng[q].dma_start(out[0], in_[0]).then_inc(T.sem[sem], 16)
+        total[sem] = 16
+        note(q, (sem, 16, dict(know[q])), in_[1], out[1])
+
+    def ext(ap):
+        return (ap, [], [])
+
+    def arrive(sem, n, *specs):
+        total[sem] = n
+        for sp in specs:
+            note("far", (sem, n, {}), [], sp[1])
+
+    def tt(out, a, b, op):
+        do("v", "tensor_tensor", out, a, b, op)
+
+    def ts(out, a, s1, op0, s2=None, op1=None):
+        if op1 is None:
+            do("v", "tensor_scalar", out, a, s1, None, op0)
+        else:
+            do("v", "tensor_scalar", out, a, s1, s2, op0, op1)
+
+    def cp(out, a):
+        do("v", "tensor_copy", out, a)
+
+    def act(out, a, f, **kw):
+        do("a", "activation", out, a, f, **kw)
+
+    def fill(out, c):
+        do("v", "memset", out, c)
+
+    def quant(name, a, b, tile, lo):
+        do("v", "quantize_mx", codes(name, a, b), plane(name, a, b), v2(tile, lo, lo + 4 * (b - a)), outs=2)
+
+    def mm(bank, n, l, la, r, ra, start=True, stop=True):
+        do("p", "matmul_mx", v2("ps%d" % bank, 0, n), codes(l, la, la + 128), plane(l, la, la + 128),
+           codes(r, ra, ra + n), plane(r, ra, ra + n), start, stop)
+
+    def iota(out, pattern, base, cm, flag=True):
+        if flag:
+            do("g", "iota", out, pattern, base, cm, allow_small_or_imprecise_dtypes=True)
+        else:
+            do("g", "iota", out, pattern, base, cm)
+
+    off = [r for r in range(N) if r != rank and topo.chip(T.cores[r]) != topo.chip(core)]
+    near = [r for r in range(N) if r != rank and topo.chip(T.cores[r]) == topo.chip(core)]
+    perm = off + near + [rank]
+    share, used, mask = 4, [], {}
+    for r in off + near:
+        es = [e for e in topo.engines(core, T.cores[r]) if e not in used][:share]
+        used += es
+        mask[r] = sum(1 << e for e in es)
+    sent = [0]
+
+    def send(ks, sem, pairs):
+        trs = []
+        for k, (src, dst) in zip(ks, pairs):
+            touch("g", src[1], [])
+            rid, pid = topo.addr(T.cores[perm[k]])[:2]
+            trs.append(RemoteDMATransfer(dst_ids=[DstId(rid=rid, pnc=pid)], dma_engine_mask=mask[perm[k]],
+                                         remote_sem=T.sem[sem], src=src[0], dst=dst[0]))
+            sent[0] += share
+        g.remote_dma_fused(trs, local_sem=T.sem.sent)
+
+    def send_cols(ks, sem, slot, land):
+        u8 = dt.uint8
+        send(ks, sem, [(codes(slot, 128 * k, 128 * k + 128, u8), codes(land, 128 * rank, 128 * rank + 128, u8)) for k in ks])
+        send(ks, sem, [(plane(slot, 128 * k, 128 * k + 128), plane(land, 128 * rank, 128 * rank + 128)) for k in ks])
+
+    far_ks, near_ks = list(range(len(off))), list(range(len(off), N - 1))
+
+    dma("s", "lpl", v2("plb", 0, 8), ext(T.pl[:, 0:8]))
+    dma("a", "lx1", v2("xb", 512, 1024), ext(T.x[:, 512:1024]))
+    dma("s", "lx0", v2("xb", 0, 512), ext(T.x[:, 0:512]))
+    dma("a", "lp2", v2("p2b", 0, 8), ext(T.p2[:, 0:8]))
+    touch("s", v2("xb", 0, 1024)[1], [])
+    dma("s", "lwv", v2("wvb", 0, 2048), ext(T.wv[:]))
+    dma("s", "lw", v2("wb", 0, 512), ext(T.w[:]))
+
+    iota(one("pc"), [[0, 1]], 0, 1, False)
+    iota(v2("sg0", 0, 18), [[0, 9], [2, 2]], -1, 0)
+    iota(v2("sg1", 0, 20), [[0, 5], [2, 2], [0, 2]], -1, 0)
+    iota(v2("vb1", 0, 128), [[32, 8], [1, 16]], -128, 0)
+    iota(v2("ctb", 0, 32), [[1, 4], [64, 8]], 0, 0)
+    iota(v2("plc", 0, 256), [[32, 4], [128, 4], [1, 16]], -256, 0)
+    iota(v2("pib", 0, 256), [[2, 4], [8, 4], [32, 16]], -256, 0)
+    iota(v2("j8", 0, 128), [[0, 16], [1, 8]], 0, 0)
+    iota(v2("c8", 0, 32), [[0, 4], [1, 8]], 0, 0)
+    iota(v2("q16", 0, 64), [[0, 4], [1, 16]], 0, 0)
+    iota(v3("dumpc", 0, 4, 0, 4), [[64, 4], [16, 4]], 2048, 1)
+    iota(v2("io2", 0, 128), [[2, 128]], 0, 0)
+    iota(v2("nadd", 0, 32), [[256, 4], [0, 8]], 1, 0)
+
+    fill(v2("w1t", 0, 1024), 0.0)
+    fill(v2("zt", 0, 512), 0.0)
+    fill(v2("zf", 0, 256), 0.0)
+    for d in range(N):
+        fill(v2("win1", 256 * d, 256 * d + 128), 128.0)
+    for n, sh, m in (("b3", 3, 1), ("b4", 4, 1), ("bb", 3, 3), ("qi", 0, 15), ("gi", 4, 7), ("oi", 0, 1), ("ji", 0, 7)):
+        ts(one(n), one("pc"), sh, A.arith_shift_right, m, A.bitwise_and)
+    ts(one("thr"), one("b3"), -TINY, A.mult, TINY, A.add)
+    tt(one("bd"), one("b4"), one("b3"), A.subtract)
+    ts(one("init1"), one("bb"), 256.0, A.mult, -1.0, A.add)
+    ts(one("h16"), one("b4"), 16.0, A.mult)
+    ts(one("bias"), one("bd"), TINY, A.mult)
+    quant("xq", 256, 384, "zt", 0)
+    for b in range(2):
+        for t in range(4):
+            ts(v2("w1t", 512 * b + t, 512 * b + 512, 32), v2("sg%d" % b, 0, 16), v2("plb", 4 * b + t, 4 * b + t + 1), A.mult)
+    quant("w1", 0, 256, "w1t", 0)
+    ts(v2("val1", 0, 128), v2("vb1", 0, 128), one("h16"), A.add)
+
+    quant("xq", 0, 256, "xb", 0)
+    mm(1, 256, "w1", 128, "xq", 0)
+    mm(0, 256, "w1", 0, "xq", 0)
+    act(v2("u1", 0, 256), v2("ps1", 0, 256), ACT.Identity, bias=one("bias"))
+    tt(v2("mz1", 0, 256), v2("ps0", 0, 256), v2("u1", 0, 256), A.max)
+    ts(v2("ind1", 0, 256), v2("mz1", 0, 256), one("thr"), A.is_lt)
+    do("v", "tensor_tensor_scan", v2("C1", 0, 256), v2("ind1", 0, 256), v2("zf", 0, 256), one("init1"), A.add, A.add)
+    tt(v2("M1", 0, 256), v2("C1", 0, 256), v2("ind1", 0, 256), A.mult)
+    do("v", "transpose", v3("t13", 0, 8, 0, 32), v2("M1", 0, 256))
+    tt(v3("u13", 0, 8, 0, 2), v3("t13", 0, 8, 0, 16, 8), v3("t13", 0, 8, 16, 32, 8), A.add)
+    tt(v2("df1", 0, 8), v3i("u13", 0, 8, 0), v3i("u13", 0, 8, 1), A.add)
+    cp(v2("do1", 0, 8), v2("df1", 0, 8))
+    cp(by(v2("win1", 0, 1024), v2("do1", 0, 8)), v2("val1", 0, 128))
+
+    def lists(half, win, stride, wd, t2):
+        a, b = 16 * half, 16 * half + 16
+        for k in (2 * half, 2 * half + 1):
+            for h in range(2):
+                cp(v3(wd, 8 * k, 8 * k + 8, 16 * h, 16 * h + 16), v2(win, stride * perm[k], stride * perm[k] + 128))
+        do("v", "transpose", v3(t2, a, b, 0, 32), v3(wd, a, b, 0, 32))
+
+    def pick(dst, a, b, src, w, offs, k):
+        o = v2(offs, 8 * k, 8 * k + (b - a) // 16)
+        cp(codes(dst, a, b, dt.uint32), by(codes(src, 0, w, dt.uint32), o))
+        act(plane(dst, a, b), by(plane(src, 0, w), o), ACT.Copy)
+
+    for half in range(2):
+        a, b = 16 * half, 16 * half + 16
+        lists(half, "win1", 256, "wd1", "t21")
+        tt(v2("l1", a, b), v3i("t21", a, b, 0), v3i("t21", a, b, 16), A.add)
+        cp(v2("off1", a, b), v2("l1", a, b))
+        ks = far_ks if half == 0 else near_ks
+        send(ks, "n1", [(v2("off1", 8 * k, 8 * k + 8), v2("nl", 8 * rank, 8 * rank + 8)) for k in ks])
+        if half == 0:
+            pick("slota", 0, 256, "xq", 384, "off1", 0)
+        else:
+            pick("slota", 256, 384, "xq", 384, "off1", 2)
+        send_cols(ks, "c1", "slota", "landa")
+    pick("landa", 128 * rank, 128 * rank + 128, "xq", 384, "off1", 3)
+    cp(v2("nl", 8 * rank, 8 * rank + 8), v2("off1", 24, 32))
+
+    ts(one("q4"), one("qi"), 4.0, A.mult)
+    ts(v2("ctf", 0, 32), v2("ctb", 0, 32), one("q4"), A.add)
+    cp(v2("offct", 0, 32), v2("ctf", 0, 32))
+    quant("wvq", 0, 512, "wvb", 0)
+    fill(v2("X", 0, 32), 0.0)
+    fill(v2("tabrow", 512, 520), 0.0)
+    fill(v2("w2t", 0, 1088), 0.0)
+    for b in range(2):
+        for t in range(4):
+            ts(v2("w2t", 544 * b + 28 + t, 544 * b + 540, 32), v2("sg%d" % b, 0, 16), v2("p2b", 4 * b + t, 4 * b + t + 1), A.mult)
+    for d in range(N):
+        fill(v2("win2", 512 * d, 512 * d + 128), 256.0)
+    quant("w2", 0, 136, "w2t", 0)
+    quant("w2", 136, 272, "w2t", 544)
+    cp(one("oddf"), one("oi"))
+    ts(one("evf"), one("oi"), -1.0, A.mult, 1.0, A.add)
+    ts(one("t15"), one("oi"), -15.0, A.mult, 16.0, A.add)
+    ts(one("t512"), one("bb"), 512.0, A.mult, -1.0, A.add)
+    ts(one("j0"), one("ji"), 0.0, A.is_equal)
+    cp(one("qf"), one("qi"))
+    cp(one("gf"), one("gi"))
+    tt(one("hc"), one("t15"), one("b4"), A.mult)
+    tt(one("init2"), one("t512"), one("j0"), A.mult)
+    act(v2("va", 0, 256), v2("plc", 0, 256), ACT.Identity, bias=one("hc"), scale=one("evf"))
+    act(v2("vp", 0, 256), v2("pib", 0, 256), ACT.Copy, scale=one("oddf"))
+    ts(v2("d0", 0, 128), v2("j8", 0, 128), 1.0, A.not_equal)
+    tt(v2("val2", 0, 256), v2("va", 0, 256), v2("vp", 0, 256), A.add)
+    ts(v2("dm1", 0, 32), v2("c8", 0, 32), one("gf"), A.is_equal)
+    ts(v2("dm2", 0, 64), v2("q16", 0, 64), one("qf"), A.is_equal)
+    quant("hq", 512, 640, "zt", 0)
+    quant("wq", 0, 128, "wb", 0)
+
+    for s in range(N):
+        if s != rank:
+            arrive("c1", 2 * share * (N - 1), codes("landa", 128 * s, 128 * s + 128), plane("landa", 128 * s, 128 * s + 128))
+            arrive("n1", share * (N - 1), v2("nl", 8 * s, 8 * s + 8))
+    for t in range(4):
+        pick("ct", 128 * t, 128 * t + 128, "landa", 512, "offct", t)
+    for t in range(4):
+        mm(t, 512, "ct", 128 * t, "wvq", 0)
+        if t < 3:
+            act(v2("vt", t, 2048, 4), v2("ps%d" % t, 0, 512), ACT.Copy)
+
+    ts(v2("fF", 0, 32), v2("nl", 0, 32), 255.5, A.is_lt)
+    cp(v2("nf", 0, 32), v2("nl", 0, 32))
+    for m in range(4):
+        do("v", "tensor_reduce", v2("X", 1 + 2 * m, 2 + 2 * m), v2("fF", 8 * m, 8 * m + 8), AxisListType.X, A.add)
+    tt(v2("nt", 0, 32), v2("nf", 0, 32), v2("nadd", 0, 32), A.add)
+    for d in range(1, 4):
+        cp(v2("X", 8 * d + 1, 8 * d + 8, 2), v2("X", 1, 8, 2))
+    do("v", "transpose", v2("xt", 0, 32), v2("X", 0, 32))
+    do("v", "tensor_reduce", one("cnt2"), v2("xt", 0, 32), AxisListType.X, A.add)
+    ts(v2("te", 0, 128), v2("io2", 0, 128), one("cnt2"), A.is_ge, LOW, A.mult)
+    ts(v2("thrm", 0, 128), v2("te", 0, 128), one("thr"), A.add)
+    dma("s", "ltb", (T.tabrow[0:1, 0:512], v2("tabrow", 0, 512)[1], []), (T.nt[0:16, 0:32], v2("nt", 0, 32)[1], []))
+    do("g", "partition_broadcast", v2("tab", 0, 520), (T.tabrow[0:1, 0:520], v2("tabrow", 0, 520)[1], []), 128)
+
+    cp(v2("vt", 3, 2048, 4), v2("ps3", 0, 512))
+    quant("vq", 0, 512, "vt", 0)
+    for h in range(2):
+        for t in range(4):
+            bank = 4 * (1 - h) + t
+            mm(bank, 256, "ct", 128 * t, "landa", 256 * h)
+            o, z = v2("at", 1024 * h + t, 1024 * h + 1024, 4), v2("ps%d" % bank, 0, 256)
+            if t % 2 == 0:
+                act(o, z, ACT.Relu, scale=0.0625)
+            else:
+                ts(o, z, 0.0, A.max, 0.0625, A.mult)
+        quant("aq", 256 * h, 256 * h + 256, "at", 1024 * h)
+    for h in range(2):
+        for i in range(4):
+            bank = 4 * (1 - h) + i
+            mm(bank, 256, "vq", 128 * i, "aq", 256 * h)
+            o, z = v2("ht", 1024 * h + i, 1024 * h + 1024, 4), v2("ps%d" % bank, 0, 256)
+            if i % 2 == 0:
+                act(o, z, ACT.Copy, scale=0.0625)
+            else:
+                ts(o, z, 0.0625, A.mult)
+        quant("hq", 256 * h, 256 * h + 256, "ht", 1024 * h)
+    for h in range(2):
+        for b in (1, 0):
+            for m in (2 * h, 2 * h + 1):
+                mm(4 + b, 128, "w2", 136 * b + 6 - 2 * m, "hq", 128 * m, m == 0, m == 3)
+
+    f128 = lambda n: v2(n, 0, 128)
+    act(f128("u2"), f128("ps5"), ACT.Identity, bias=one("bias"))
+    tt(f128("mz2"), f128("ps4"), f128("u2"), A.max)
+    tt(f128("ind2"), f128("mz2"), f128("thrm"), A.is_lt)
+    act(f128("pen"), f128("ind2"), ACT.Copy, bias=FAR, scale=-FAR)
+    do("v", "tensor_tensor_scan", f128("C2"), f128("ind2"), f128("zf"), one("init2"), A.add, A.add)
+    act(v2("mb", 128, 256), f128("zf"), ACT.Identity, bias=v2("C2", 127, 128))
+    tt(f128("mb"), f128("C2"), f128("pen"), A.add)
+    do("v", "transpose", v2("tt", 0, 256), v2("mb", 0, 256))
+    do("v", "tensor_tensor_scan", f128("base"), f128("d0"), v2("tt", 127, 255), 0.0, A.mult, A.add)
+    tt(v3("D3", 0, 4, 0, 32), f128("tt"), f128("base"), A.add)
+    tt(v3("E3", 0, 4, 0, 16), v3("D3", 0, 4, 0, 16), v3("D3", 0, 4, 16, 32), A.min)
+    tt(v3("F3", 0, 4, 0, 8), v3("E3", 0, 4, 0, 8), v3("E3", 0, 4, 8, 16), A.min)
+    tt(v3("dst3", 0, 4, 0, 4), v3("F3", 0, 4, 1, 8, 2), v3("dumpc", 0, 4, 0, 4), A.min)
+    cp(v2("do2", 0, 16), v3("dst3", 0, 4, 0, 4))
+    cp(by(v2("win2", 0, 2432), v2("do2", 0, 16)), v2("val2", 0, 256))
+    for half in range(2):
+        a, b = 16 * half, 16 * half + 16
+        lists(half, "win2", 512, "wd2", "t22")
+        tt(v3("l2", a, b, 0, 2), v3("t22", a, b, 0, 2), v3("t22", a, b, 16, 18), A.add)
+        cp(v2("off2", a, b), v3i("l2", a, b, 0))
+        if half == 0:
+            pick("slotb", 0, 256, "hq", 640, "off2", 0)
+        else:
+            pick("slotb", 256, 384, "hq", 640, "off2", 2)
+        send_cols(far_ks if half == 0 else near_ks, "c2_%d" % rank, "slotb", "landb")
+    tt(v2("pd", 0, 32), v3i("l2", 0, 32, 1), v2("dm1", 0, 32), A.mult)
+    for k in range(4):
+        do("v", "tensor_reduce", v2("pdr", k, k + 1), v2("pd", 8 * k, 8 * k + 8), AxisListType.X, A.add)
+    cp(v2("offD", 0, 4), v2("pdr", 0, 4))
+    cp(v2("ga", 0, 64), by(v2("tab", 0, 520), v2("offD", 0, 4)))
+    tt(v2("gm", 0, 64), v2("ga", 0, 64), v2("dm2", 0, 64), A.mult)
+    for k in range(4):
+        do("v", "tensor_reduce", v2("idr", k, k + 1), v2("gm", 16 * k, 16 * k + 16), AxisListType.X, A.add)
+    cp(v2("idu", 0, 4), v2("idr", 0, 4))
+    ks = far_ks + near_ks
+    send(ks, "n2", [(v2("idu", k, k + 1), v2("idl", 8 * rank, 8 * rank + 1)) for k in ks])
+    pick("landb", 128 * rank, 128 * rank + 128, "hq", 640, "off2", 3)
+    cp(v2("idl", 8 * rank, 8 * rank + 1), v2("idr", 3, 4))
+
+    for s in range(N):
+        if s != rank:
+            arrive("c2_%d" % s, 2 * share, codes("landb", 128 * s, 128 * s + 128), plane("landb", 128 * s, 128 * s + 128))
+            arrive("n2", share * (N - 1), v2("idl", 8 * s, 8 * s + 1))
+    for i, s in enumerate([rank] + near + off):
+        bank = (6, 7, 0, 1)[i]
+        mm(bank, 128, "wq", 0, "landb", 128 * s)
+        o, z = v2("yb", 128 * s, 128 * s + 128), v2("ps%d" % bank, 0, 128)
+        if i < 3:
+            act(o, z, ACT.Copy)
+        else:
+            cp(o, z)
+        dma("s", "oc%d" % s, ext(T.oc[:, 512 * s:512 * s + 512]), codes("landb", 128 * s, 128 * s + 128, dt.uint8))
+        dma("a" if i < 3 else "s", "yy%d" % s, ext(T.y[:, 128 * s:128 * s + 128]), o)
+    for k in range(4):
+        dma("a" if k % 2 else "s", "os%d" % k, ext(T.osc[4 * k:4 * k + 4, :]),
+            (T.landbs[32 * k:32 * k + 4, 0:512], plane("landb", 0, 512)[1], []))
+    ts(v2("idf", 0, 4), v2("idl", 0, 32, 8), -1.0, A.add)
+    for s in range(N):
+        dma("a" if s % 2 else "s", "ii%d" % s, ext(T["id"][0:1, 128 * s:128 * s + 128]), v2("idf", s, s + 1))
+    total["sent"] = sent[0]
+    for sem in SEMAPHORES:
+        if total.get(sem, 0) > waited.get(sem, 0):
+            g.wait_ge(T.sem[sem], total[sem])

@@ -8,9 +8,9 @@ COL.update({n: ("kf", k) for k, n in enumerate((
     "thr", "bd", "bias", "init1", "h16", "q4", "qf", "gf", "oddf", "evf", "t15", "hc", "t512", "j0", "init2", "cnt2"))})
 SCRATCH = {}
 for _n, _w, _t in (
-        ("plb", 8, B), ("p2b", 8, B), ("xb", 1024, B), ("wvb", 2048, B), ("wb", 512, B),
+        ("plb", 8, B), ("p2b", 8, B), ("p2f", 8, F), ("xb", 1024, B), ("wvb", 2048, B), ("wb", 512, B),
         ("w1t", 1024, B), ("zt", 512, B), ("w2t", 1088, B), ("at", 2048, B), ("vt", 2048, B), ("ht", 2048, B),
-        ("sg0", 20, B), ("sg1", 20, B), ("val1", 128, B), ("val2", 256, B), ("win1", 1024, B), ("win2", 2432, B),
+        ("sg0", 128, B), ("sg1", 128, B), ("val1", 128, B), ("val2", 256, B), ("win1", 1024, B), ("win2", 2432, B),
         ("ki", 8, I), ("kf", 16, F),
         ("vb1", 128, F), ("ctb", 32, F), ("ctf", 32, F), ("j8", 128, F), ("d0", 128, F), ("plc", 256, F), ("pib", 256, F),
         ("va", 256, F), ("vp", 256, F), ("c8", 32, F), ("dm1", 32, F), ("q16", 64, F), ("dm2", 64, F), ("io2", 128, F),
@@ -18,8 +18,8 @@ for _n, _w, _t in (
         ("te", 128, F), ("thrm", 128, F), ("tabrow", 520, F), ("tab", 520, F),
         ("u1", 256, F), ("mz1", 256, F), ("ind1", 256, F), ("C1", 256, F), ("M1", 256, F), ("df1", 8, F), ("l1", 32, F),
         ("u2", 128, F), ("mz2", 128, F), ("ind2", 128, F), ("C2", 128, F), ("pen", 128, F), ("mb", 256, F), ("tt", 256, F),
-        ("base", 128, F), ("pd", 32, F), ("pdr", 4, F), ("ga", 64, F), ("gm", 64, F), ("idr", 4, F), ("idf", 4, F),
-        ("yb", 512, F),
+        ("base", 128, F), ("pd", 32, F), ("pdr", 4, F), ("ga", 64, F), ("gm", 64, F), ("idr", 4, F), ("idp", 32, F),
+        ("idt", 32, F), ("yb", 512, F),
         ("do1", 8, U), ("do2", 16, U), ("off1", 32, U), ("off2", 32, U), ("offct", 32, U), ("offD", 4, U), ("nl", 32, U),
         ("idu", 4, U), ("idl", 32, U)):
     SCRATCH[_n] = ("sbuf", [128, _w], _t)
@@ -172,6 +172,9 @@ def rank_program(g, core, T, topo):
     def fill(out, c):
         do("v", "memset", out, c)
 
+    def total_of(out, a):
+        do("v", "tensor_reduce", out, a, AxisListType.X, A.add)
+
     def quant(name, a, b, tile, lo):
         do("v", "quantize_mx", codes(name, a, b), plane(name, a, b), v2(tile, lo, lo + 4 * (b - a)), outs=2)
 
@@ -188,9 +191,11 @@ def rank_program(g, core, T, topo):
     off = [r for r in range(N) if r != rank and topo.chip(T.cores[r]) != topo.chip(core)]
     near = [r for r in range(N) if r != rank and topo.chip(T.cores[r]) == topo.chip(core)]
     perm = off + near + [rank]
-    share, used, mask = 4, [], {}
+    share = {r: 8 if r in near else 4 for r in off + near}
+    every = sum(share.values())
+    used, mask = [], {}
     for r in off + near:
-        es = [e for e in topo.engines(core, T.cores[r]) if e not in used][:share]
+        es = [e for e in topo.engines(core, T.cores[r]) if e not in used][:share[r]]
         used += es
         mask[r] = sum(1 << e for e in es)
     sent = [0]
@@ -202,7 +207,7 @@ def rank_program(g, core, T, topo):
             rid, pid = topo.addr(T.cores[perm[k]])[:2]
             trs.append(RemoteDMATransfer(dst_ids=[DstId(rid=rid, pnc=pid)], dma_engine_mask=mask[perm[k]],
                                          remote_sem=T.sem[sem], src=src[0], dst=dst[0]))
-            sent[0] += share
+            sent[0] += share[perm[k]]
         g.remote_dma_fused(trs, local_sem=T.sem.sent)
 
     def send_cols(ks, sem, slot, land):
@@ -211,18 +216,19 @@ def rank_program(g, core, T, topo):
         send(ks, sem, [(plane(slot, 128 * k, 128 * k + 128), plane(land, 128 * rank, 128 * rank + 128)) for k in ks])
 
     far_ks, near_ks = list(range(len(off))), list(range(len(off), N - 1))
+    all_ks = far_ks + near_ks
 
     dma("s", "lpl", v2("plb", 0, 8), ext(T.pl[:, 0:8]))
     dma("a", "lx1", v2("xb", 512, 1024), ext(T.x[:, 512:1024]))
     dma("s", "lx0", v2("xb", 0, 512), ext(T.x[:, 0:512]))
-    dma("a", "lp2", v2("p2b", 0, 8), ext(T.p2[:, 0:8]))
     touch("s", v2("xb", 0, 1024)[1], [])
+    dma("s", "lp2", v2("p2b", 0, 8), ext(T.p2[:, 0:8]))
     dma("s", "lwv", v2("wvb", 0, 2048), ext(T.wv[:]))
     dma("s", "lw", v2("wb", 0, 512), ext(T.w[:]))
 
     iota(one("pc"), [[0, 1]], 0, 1, False)
-    iota(v2("sg0", 0, 18), [[0, 9], [2, 2]], -1, 0)
-    iota(v2("sg1", 0, 20), [[0, 5], [2, 2], [0, 2]], -1, 0)
+    iota(v2("sg1", 0, 128), [[0, 4], [2, 2], [0, 16]], -1, 0)
+    iota(v2("sg0", 0, 128), [[0, 8], [2, 2], [0, 8]], -1, 0)
     iota(v2("vb1", 0, 128), [[32, 8], [1, 16]], -128, 0)
     iota(v2("ctb", 0, 32), [[1, 4], [64, 8]], 0, 0)
     iota(v2("plc", 0, 256), [[32, 4], [128, 4], [1, 16]], -256, 0)
@@ -233,30 +239,32 @@ def rank_program(g, core, T, topo):
     iota(v3("dumpc", 0, 4, 0, 4), [[64, 4], [16, 4]], 2048, 1)
     iota(v2("io2", 0, 128), [[2, 128]], 0, 0)
     iota(v2("nadd", 0, 32), [[256, 4], [0, 8]], 1, 0)
+    iota(v2("w2t", 0, 1088), [[0, 1088]], 0, 0)
 
-    fill(v2("w1t", 0, 1024), 0.0)
     fill(v2("zt", 0, 512), 0.0)
-    fill(v2("zf", 0, 256), 0.0)
-    for d in range(N):
-        fill(v2("win1", 256 * d, 256 * d + 128), 128.0)
-    for n, sh, m in (("b3", 3, 1), ("b4", 4, 1), ("bb", 3, 3), ("qi", 0, 15), ("gi", 4, 7), ("oi", 0, 1), ("ji", 0, 7)):
+    for n, sh, m in (("b3", 3, 1), ("b4", 4, 1), ("bb", 3, 3)):
         ts(one(n), one("pc"), sh, A.arith_shift_right, m, A.bitwise_and)
     ts(one("thr"), one("b3"), -TINY, A.mult, TINY, A.add)
     tt(one("bd"), one("b4"), one("b3"), A.subtract)
     ts(one("init1"), one("bb"), 256.0, A.mult, -1.0, A.add)
     ts(one("h16"), one("b4"), 16.0, A.mult)
     ts(one("bias"), one("bd"), TINY, A.mult)
-    quant("xq", 256, 384, "zt", 0)
-    for b in range(2):
-        for t in range(4):
-            ts(v2("w1t", 512 * b + t, 512 * b + 512, 32), v2("sg%d" % b, 0, 16), v2("plb", 4 * b + t, 4 * b + t + 1), A.mult)
-    quant("w1", 0, 256, "w1t", 0)
+    fill(v2("zf", 0, 256), 0.0)
     ts(v2("val1", 0, 128), v2("vb1", 0, 128), one("h16"), A.add)
+    for d in range(N):
+        fill(v2("win1", 256 * d, 256 * d + 128), 128.0)
+    quant("xq", 256, 384, "zt", 0)
+    for b in (1, 0):
+        for t in range(4):
+            ts(v2("w1t", 512 * b + t, 512 * b + 512, 4), v2("sg%d" % b, 0, 128), v2("plb", 4 * b + t, 4 * b + t + 1), A.mult)
+        if b == 1:
+            quant("w1", 128, 256, "w1t", 512)
 
     quant("xq", 0, 256, "xb", 0)
+    quant("w1", 0, 128, "w1t", 0)
     mm(1, 256, "w1", 128, "xq", 0)
     mm(0, 256, "w1", 0, "xq", 0)
-    act(v2("u1", 0, 256), v2("ps1", 0, 256), ACT.Identity, bias=one("bias"))
+    ts(v2("u1", 0, 256), v2("ps1", 0, 256), one("bias"), A.add)
     tt(v2("mz1", 0, 256), v2("ps0", 0, 256), v2("u1", 0, 256), A.max)
     ts(v2("ind1", 0, 256), v2("mz1", 0, 256), one("thr"), A.is_lt)
     do("v", "tensor_tensor_scan", v2("C1", 0, 256), v2("ind1", 0, 256), v2("zf", 0, 256), one("init1"), A.add, A.add)
@@ -284,85 +292,81 @@ def rank_program(g, core, T, topo):
         lists(half, "win1", 256, "wd1", "t21")
         tt(v2("l1", a, b), v3i("t21", a, b, 0), v3i("t21", a, b, 16), A.add)
         cp(v2("off1", a, b), v2("l1", a, b))
-        ks = far_ks if half == 0 else near_ks
-        send(ks, "n1", [(v2("off1", 8 * k, 8 * k + 8), v2("nl", 8 * rank, 8 * rank + 8)) for k in ks])
         if half == 0:
             pick("slota", 0, 256, "xq", 384, "off1", 0)
         else:
             pick("slota", 256, 384, "xq", 384, "off1", 2)
-        send_cols(ks, "c1", "slota", "landa")
+        send_cols(far_ks if half == 0 else near_ks, "c1", "slota", "landa")
+    send(all_ks, "n1", [(v2("off1", 8 * k, 8 * k + 8), v2("nl", 8 * rank, 8 * rank + 8)) for k in all_ks])
     pick("landa", 128 * rank, 128 * rank + 128, "xq", 384, "off1", 3)
     cp(v2("nl", 8 * rank, 8 * rank + 8), v2("off1", 24, 32))
 
-    ts(one("q4"), one("qi"), 4.0, A.mult)
-    ts(v2("ctf", 0, 32), v2("ctb", 0, 32), one("q4"), A.add)
-    cp(v2("offct", 0, 32), v2("ctf", 0, 32))
-    quant("wvq", 0, 512, "wvb", 0)
-    fill(v2("X", 0, 32), 0.0)
-    fill(v2("tabrow", 512, 520), 0.0)
-    fill(v2("w2t", 0, 1088), 0.0)
+    for d in range(N):
+        iota(v2("win2", 512 * d, 512 * d + 128), [[0, 128]], 256, 0)
+    act(v2("p2f", 0, 8), v2("p2b", 0, 8), ACT.Copy)
     for b in range(2):
         for t in range(4):
-            ts(v2("w2t", 544 * b + 28 + t, 544 * b + 540, 32), v2("sg%d" % b, 0, 16), v2("p2b", 4 * b + t, 4 * b + t + 1), A.mult)
-    for d in range(N):
-        fill(v2("win2", 512 * d, 512 * d + 128), 256.0)
-    quant("w2", 0, 136, "w2t", 0)
-    quant("w2", 136, 272, "w2t", 544)
-    cp(one("oddf"), one("oi"))
+            act(v2("w2t", 544 * b + 28 + t, 544 * b + 540, 32), v2("sg%d" % b, 0, 128, 8), ACT.Copy,
+                scale=v2("p2f", 4 * b + t, 4 * b + t + 1))
+    for n, sh, m in (("qi", 0, 15), ("gi", 4, 7), ("oi", 0, 1), ("ji", 0, 7)):
+        ts(one(n), one("pc"), sh, A.arith_shift_right, m, A.bitwise_and)
+    ts(one("q4"), one("qi"), 4.0, A.mult)
     ts(one("evf"), one("oi"), -1.0, A.mult, 1.0, A.add)
     ts(one("t15"), one("oi"), -15.0, A.mult, 16.0, A.add)
+    cp(one("oddf"), one("oi"))
+    ts(v2("ctf", 0, 32), v2("ctb", 0, 32), one("q4"), A.add)
+    tt(one("hc"), one("t15"), one("b4"), A.mult)
+    cp(v2("offct", 0, 32), v2("ctf", 0, 32))
+    act(v2("va", 0, 256), v2("plc", 0, 256), ACT.Identity, bias=one("hc"), scale=one("evf"))
+    act(v2("vp", 0, 256), v2("pib", 0, 256), ACT.Copy, scale=one("oddf"))
+    quant("wvq", 0, 512, "wvb", 0)
     ts(one("t512"), one("bb"), 512.0, A.mult, -1.0, A.add)
     ts(one("j0"), one("ji"), 0.0, A.is_equal)
     cp(one("qf"), one("qi"))
     cp(one("gf"), one("gi"))
-    tt(one("hc"), one("t15"), one("b4"), A.mult)
     tt(one("init2"), one("t512"), one("j0"), A.mult)
-    act(v2("va", 0, 256), v2("plc", 0, 256), ACT.Identity, bias=one("hc"), scale=one("evf"))
-    act(v2("vp", 0, 256), v2("pib", 0, 256), ACT.Copy, scale=one("oddf"))
+    fill(v2("X", 0, 32), 0.0)
+    fill(v2("X", 9, 32, 2), 8.0)
+    fill(v2("tabrow", 512, 520), 0.0)
+    fill(v2("idp", 0, 32), 0.0)
+    quant("hq", 512, 640, "zt", 0)
     ts(v2("d0", 0, 128), v2("j8", 0, 128), 1.0, A.not_equal)
-    tt(v2("val2", 0, 256), v2("va", 0, 256), v2("vp", 0, 256), A.add)
     ts(v2("dm1", 0, 32), v2("c8", 0, 32), one("gf"), A.is_equal)
     ts(v2("dm2", 0, 64), v2("q16", 0, 64), one("qf"), A.is_equal)
-    quant("hq", 512, 640, "zt", 0)
-    quant("wq", 0, 128, "wb", 0)
+    tt(v2("val2", 0, 256), v2("va", 0, 256), v2("vp", 0, 256), A.add)
 
     for s in range(N):
         if s != rank:
-            arrive("c1", 2 * share * (N - 1), codes("landa", 128 * s, 128 * s + 128), plane("landa", 128 * s, 128 * s + 128))
-            arrive("n1", share * (N - 1), v2("nl", 8 * s, 8 * s + 8))
+            arrive("c1", 2 * every, codes("landa", 128 * s, 128 * s + 128), plane("landa", 128 * s, 128 * s + 128))
+            arrive("n1", every, v2("nl", 8 * s, 8 * s + 8))
     for t in range(4):
         pick("ct", 128 * t, 128 * t + 128, "landa", 512, "offct", t)
+    quant("w2", 0, 136, "w2t", 0)
+    quant("w2", 136, 272, "w2t", 544)
     for t in range(4):
         mm(t, 512, "ct", 128 * t, "wvq", 0)
-        if t < 3:
-            act(v2("vt", t, 2048, 4), v2("ps%d" % t, 0, 512), ACT.Copy)
-
-    ts(v2("fF", 0, 32), v2("nl", 0, 32), 255.5, A.is_lt)
-    cp(v2("nf", 0, 32), v2("nl", 0, 32))
-    for m in range(4):
-        do("v", "tensor_reduce", v2("X", 1 + 2 * m, 2 + 2 * m), v2("fF", 8 * m, 8 * m + 8), AxisListType.X, A.add)
-    tt(v2("nt", 0, 32), v2("nf", 0, 32), v2("nadd", 0, 32), A.add)
-    for d in range(1, 4):
-        cp(v2("X", 8 * d + 1, 8 * d + 8, 2), v2("X", 1, 8, 2))
-    do("v", "transpose", v2("xt", 0, 32), v2("X", 0, 32))
-    do("v", "tensor_reduce", one("cnt2"), v2("xt", 0, 32), AxisListType.X, A.add)
-    ts(v2("te", 0, 128), v2("io2", 0, 128), one("cnt2"), A.is_ge, LOW, A.mult)
-    ts(v2("thrm", 0, 128), v2("te", 0, 128), one("thr"), A.add)
-    dma("s", "ltb", (T.tabrow[0:1, 0:512], v2("tabrow", 0, 512)[1], []), (T.nt[0:16, 0:32], v2("nt", 0, 32)[1], []))
-    do("g", "partition_broadcast", v2("tab", 0, 520), (T.tabrow[0:1, 0:520], v2("tabrow", 0, 520)[1], []), 128)
-
-    cp(v2("vt", 3, 2048, 4), v2("ps3", 0, 512))
+        o, z = v2("vt", t, 2048, 4), v2("ps%d" % t, 0, 512)
+        if t % 2 == 0:
+            act(o, z, ACT.Copy)
+        else:
+            cp(o, z)
+        if t == 1:
+            ts(v2("fF", 0, 32), v2("nl", 0, 32), 255.5, A.is_lt)
+            for m in range(4):
+                total_of(v2("X", 1 + 2 * m, 2 + 2 * m), v2("fF", 8 * m, 8 * m + 8))
     quant("vq", 0, 512, "vt", 0)
     for h in range(2):
         for t in range(4):
             bank = 4 * (1 - h) + t
             mm(bank, 256, "ct", 128 * t, "landa", 256 * h)
             o, z = v2("at", 1024 * h + t, 1024 * h + 1024, 4), v2("ps%d" % bank, 0, 256)
-            if t % 2 == 0:
-                act(o, z, ACT.Relu, scale=0.0625)
-            else:
+            if t == 3 or (h == 1 and t == 1):
                 ts(o, z, 0.0, A.max, 0.0625, A.mult)
+            else:
+                act(o, z, ACT.Relu, scale=0.0625)
         quant("aq", 256 * h, 256 * h + 256, "at", 1024 * h)
+    do("v", "transpose", v2("xt", 0, 32), v2("X", 0, 32))
+    total_of(one("cnt2"), v2("xt", 0, 32))
     for h in range(2):
         for i in range(4):
             bank = 4 * (1 - h) + i
@@ -379,12 +383,18 @@ def rank_program(g, core, T, topo):
                 mm(4 + b, 128, "w2", 136 * b + 6 - 2 * m, "hq", 128 * m, m == 0, m == 3)
 
     f128 = lambda n: v2(n, 0, 128)
-    act(f128("u2"), f128("ps5"), ACT.Identity, bias=one("bias"))
+    ts(f128("te"), f128("io2"), one("cnt2"), A.is_ge, LOW, A.mult)
+    ts(f128("thrm"), f128("te"), one("thr"), A.add)
+    cp(v2("nf", 0, 32), v2("nl", 0, 32))
+    tt(v2("nt", 0, 32), v2("nf", 0, 32), v2("nadd", 0, 32), A.add)
+    dma("s", "ltb", (T.tabrow[0:1, 0:512], v2("tabrow", 0, 512)[1], []), (T.nt[0:16, 0:32], v2("nt", 0, 32)[1], []))
+    do("g", "partition_broadcast", v2("tab", 0, 520), (T.tabrow[0:1, 0:520], v2("tabrow", 0, 520)[1], []), 128)
+    ts(f128("u2"), f128("ps5"), one("bias"), A.add)
     tt(f128("mz2"), f128("ps4"), f128("u2"), A.max)
     tt(f128("ind2"), f128("mz2"), f128("thrm"), A.is_lt)
-    act(f128("pen"), f128("ind2"), ACT.Copy, bias=FAR, scale=-FAR)
     do("v", "tensor_tensor_scan", f128("C2"), f128("ind2"), f128("zf"), one("init2"), A.add, A.add)
     act(v2("mb", 128, 256), f128("zf"), ACT.Identity, bias=v2("C2", 127, 128))
+    ts(f128("pen"), f128("ind2"), -FAR, A.mult, FAR, A.add)
     tt(f128("mb"), f128("C2"), f128("pen"), A.add)
     do("v", "transpose", v2("tt", 0, 256), v2("mb", 0, 256))
     do("v", "tensor_tensor_scan", f128("base"), f128("d0"), v2("tt", 127, 255), 0.0, A.mult, A.add)
@@ -406,23 +416,24 @@ def rank_program(g, core, T, topo):
         send_cols(far_ks if half == 0 else near_ks, "c2_%d" % rank, "slotb", "landb")
     tt(v2("pd", 0, 32), v3i("l2", 0, 32, 1), v2("dm1", 0, 32), A.mult)
     for k in range(4):
-        do("v", "tensor_reduce", v2("pdr", k, k + 1), v2("pd", 8 * k, 8 * k + 8), AxisListType.X, A.add)
+        total_of(v2("pdr", k, k + 1), v2("pd", 8 * k, 8 * k + 8))
     cp(v2("offD", 0, 4), v2("pdr", 0, 4))
     cp(v2("ga", 0, 64), by(v2("tab", 0, 520), v2("offD", 0, 4)))
     tt(v2("gm", 0, 64), v2("ga", 0, 64), v2("dm2", 0, 64), A.mult)
     for k in range(4):
-        do("v", "tensor_reduce", v2("idr", k, k + 1), v2("gm", 16 * k, 16 * k + 16), AxisListType.X, A.add)
+        total_of(v2("idr", k, k + 1), v2("gm", 16 * k, 16 * k + 16))
     cp(v2("idu", 0, 4), v2("idr", 0, 4))
-    ks = far_ks + near_ks
-    send(ks, "n2", [(v2("idu", k, k + 1), v2("idl", 8 * rank, 8 * rank + 1)) for k in ks])
+    send(all_ks, "n2", [(v2("idu", k, k + 1), v2("idl", 8 * rank, 8 * rank + 1)) for k in all_ks])
     pick("landb", 128 * rank, 128 * rank + 128, "hq", 640, "off2", 3)
     cp(v2("idl", 8 * rank, 8 * rank + 1), v2("idr", 3, 4))
+    quant("wq", 0, 128, "wb", 0)
 
     for s in range(N):
         if s != rank:
-            arrive("c2_%d" % s, 2 * share, codes("landb", 128 * s, 128 * s + 128), plane("landb", 128 * s, 128 * s + 128))
-            arrive("n2", share * (N - 1), v2("idl", 8 * s, 8 * s + 1))
-    for i, s in enumerate([rank] + near + off):
+            arrive("c2_%d" % s, 2 * share[s], codes("landb", 128 * s, 128 * s + 128), plane("landb", 128 * s, 128 * s + 128))
+            arrive("n2", every, v2("idl", 8 * s, 8 * s + 1))
+    turn = [rank] + near + off
+    for i, s in enumerate(turn):
         bank = (6, 7, 0, 1)[i]
         mm(bank, 128, "wq", 0, "landb", 128 * s)
         o, z = v2("yb", 128 * s, 128 * s + 128), v2("ps%d" % bank, 0, 128)
@@ -435,9 +446,11 @@ def rank_program(g, core, T, topo):
     for k in range(4):
         dma("a" if k % 2 else "s", "os%d" % k, ext(T.osc[4 * k:4 * k + 4, :]),
             (T.landbs[32 * k:32 * k + 4, 0:512], plane("landb", 0, 512)[1], []))
-    ts(v2("idf", 0, 4), v2("idl", 0, 32, 8), -1.0, A.add)
+    ts(v2("idp", 0, 4), v2("idl", 0, 32, 8), -1.0, A.add)
+    do("v", "transpose", v2("idt", 0, 32), v2("idp", 0, 32))
     for s in range(N):
-        dma("a" if s % 2 else "s", "ii%d" % s, ext(T["id"][0:1, 128 * s:128 * s + 128]), v2("idf", s, s + 1))
+        dma("a" if s % 2 else "s", "ii%d" % s, ext(T["id"][0:1, 128 * s:128 * s + 128]),
+            (T.idt[s:128:32, 0:32], v2("idt", 0, 32)[1], []))
     total["sent"] = sent[0]
     for sem in SEMAPHORES:
         if total.get(sem, 0) > waited.get(sem, 0):

@@ -3,31 +3,34 @@ from concourse.mybir import dt, AluOpType, AxisListType, ActivationFunctionType
 
 F, B, I, U = "float32", "bfloat16", "int32", "uint16"
 Q, S8 = "float8_e4m3fn_x4", "uint8"
-COL = {n: ("ki", k) for k, n in enumerate(("pc", "b3", "b4", "bb", "qi", "gi", "oi", "ji"))}
+COL = {n: ("ki", k) for k, n in enumerate(("pc", "b3", "b4", "bb", "j3", "ji", "qi", "gi", "oi"))}
 COL.update({n: ("kf", k) for k, n in enumerate((
-    "thr", "bd", "bias", "init1", "h16", "q4", "qf", "gf", "oddf", "evf", "t15", "hc", "t512", "j0", "init2", "cnt2"))})
+    "thrm", "bias", "h16", "j0", "init1", "init2", "out1", "out2", "thr1", "thr2", "q4", "qf", "gf", "oddf", "evf",
+    "t15", "hc", "cnt2", "kk"))})
 SCRATCH = {}
 for _n, _w, _t in (
-        ("plb", 8, B), ("p2b", 8, B), ("p2f", 8, F), ("xb", 1024, B), ("wvb", 2048, B), ("wb", 512, B),
-        ("w1t", 1024, B), ("zt", 512, B), ("w2t", 1088, B), ("at", 2048, B), ("vt", 2048, B), ("ht", 2048, B),
-        ("sg0", 128, B), ("sg1", 128, B), ("val1", 128, B), ("val2", 256, B), ("win1", 1024, B), ("win2", 2432, B),
-        ("ki", 8, I), ("kf", 16, F),
-        ("vb1", 128, F), ("ctb", 32, F), ("ctf", 32, F), ("j8", 128, F), ("d0", 128, F), ("plc", 256, F), ("pib", 256, F),
-        ("va", 256, F), ("vp", 256, F), ("c8", 32, F), ("dm1", 32, F), ("q16", 64, F), ("dm2", 64, F), ("io2", 128, F),
-        ("nadd", 32, F), ("zf", 256, F), ("X", 32, F), ("xt", 32, F), ("fF", 32, F), ("nf", 32, F), ("nt", 32, F),
-        ("te", 128, F), ("thrm", 128, F), ("tabrow", 520, F), ("tab", 520, F),
-        ("u1", 256, F), ("mz1", 256, F), ("ind1", 256, F), ("C1", 256, F), ("M1", 256, F), ("df1", 8, F), ("l1", 32, F),
-        ("u2", 128, F), ("mz2", 128, F), ("ind2", 128, F), ("C2", 128, F), ("pen", 128, F), ("mb", 256, F), ("tt", 256, F),
-        ("base", 128, F), ("pd", 32, F), ("pdr", 4, F), ("ga", 64, F), ("gm", 64, F), ("idr", 4, F), ("idp", 32, F),
+        ("plb", 8, B), ("p2b", 8, B), ("p1f", 8, F), ("p2f", 8, F), ("xb", 1024, B), ("wvb", 2048, B), ("wb", 512, B),
+        ("w1t", 1088, B), ("zt", 544, B), ("w2t", 1088, B), ("at", 2048, B), ("vt", 2048, B), ("ht", 2048, B),
+        ("sg0", 16, B), ("sg1", 16, B), ("val1", 128, B), ("val2", 256, B), ("win1", 1040, B), ("win2", 2448, B),
+        ("ki", 16, I), ("kf", 24, F),
+        ("vb1", 128, F), ("ctb", 32, F), ("ctf", 32, F), ("j8", 128, B), ("d0", 128, B), ("plc", 256, F), ("pib", 256, F),
+        ("va", 256, F), ("vp", 256, F), ("c8", 32, F), ("dm1", 32, F), ("f8", 32, F), ("q16", 64, F), ("dm2", 64, F),
+        ("f16", 64, F), ("io2", 128, F), ("nadd", 32, F), ("X", 32, F), ("xt", 32, F), ("fF", 32, F), ("nf", 32, F),
+        ("nt", 32, F), ("te", 128, F), ("bm", 128, F), ("tabrow", 520, F), ("tab", 520, F),
+        ("u1", 128, F), ("mz1", 128, F), ("ind1", 256, B), ("C1", 256, B), ("tI1", 128, B), ("tC1", 256, B),
+        ("base1", 128, F), ("D1", 32, F), ("l1", 32, F),
+        ("u2", 128, F), ("mz2", 128, F), ("ind2", 256, B), ("C2", 256, B), ("tI2", 128, B), ("tC2", 256, B),
+        ("base2", 128, F), ("D2", 64, F),
+        ("pd", 32, F), ("pds", 32, F), ("ga", 64, F), ("gm", 64, F), ("gms", 64, F), ("idp", 32, F),
         ("idt", 32, F), ("yb", 512, F),
         ("do1", 8, U), ("do2", 16, U), ("off1", 32, U), ("off2", 32, U), ("offct", 32, U), ("offD", 4, U), ("nl", 32, U),
         ("idu", 4, U), ("idl", 32, U)):
     SCRATCH[_n] = ("sbuf", [128, _w], _t)
-for _n, _a, _b, _t in (("t13", 8, 32, F), ("u13", 8, 2, F), ("wd1", 32, 32, B), ("t21", 32, 32, B), ("D3", 4, 32, F),
-                       ("E3", 4, 16, F), ("F3", 4, 8, F), ("dst3", 4, 4, F), ("dumpc", 4, 4, F), ("wd2", 32, 32, B),
-                       ("t22", 32, 32, B), ("l2", 32, 2, F)):
+for _n, _a, _b, _t in (("M1", 4, 8, F), ("E1", 4, 4, F), ("F1", 4, 2, F), ("wd1", 32, 32, B), ("t21", 32, 32, B),
+                       ("M2", 4, 16, F), ("E2", 4, 8, F), ("F2", 4, 4, F), ("dst2", 4, 4, F), ("dumpc", 4, 4, F),
+                       ("wd2", 32, 32, B), ("t22", 32, 32, B), ("l2", 32, 2, F)):
     SCRATCH[_n] = ("sbuf", [128, _a, _b], _t)
-for _n, _w in (("w1", 256), ("xq", 384), ("slota", 384), ("landa", 512), ("ct", 512), ("wvq", 512), ("aq", 512), ("vq", 512),
+for _n, _w in (("w1", 272), ("xq", 384), ("slota", 384), ("landa", 512), ("ct", 512), ("wvq", 512), ("aq", 512), ("vq", 512),
                ("w2", 272), ("hq", 640), ("slotb", 384), ("landb", 512), ("wq", 128)):
     SCRATCH[_n + "c"] = ("sbuf", [128, _w], Q)
     SCRATCH[_n + "s"] = ("sbuf", [128, _w], S8)
@@ -35,11 +38,12 @@ for _k in range(8):
     SCRATCH["ps%d" % _k] = ("psum", [128, 512], F)
 
 SEMAPHORES = (["sv", "sa", "sp", "sg", "sent", "c1", "n1", "n2", "lpl", "lx0", "lx1", "lp2", "lwv", "lw", "ltb"]
-              + ["c2_%d" % k for k in range(4)] + ["%s%d" % (n, k) for n in ("oc", "os", "yy", "ii") for k in range(4)])
+              + ["%s_%d" % (n, k) for n in ("c2", "s2") for k in range(4)]
+              + ["%s%d" % (n, k) for n in ("oc", "os", "yy", "ii") for k in range(4)])
 
 TINY = 2.0 ** -120
-FAR = 8192.0
-LOW = -2.0 ** 99
+LOW, HIGH = -2.0 ** 99, 2.0 ** 99
+DUMP = 384
 
 
 def rank_program(g, core, T, topo):
@@ -172,6 +176,12 @@ def rank_program(g, core, T, topo):
     def fill(out, c):
         do("v", "memset", out, c)
 
+    def scan(out, a, b, init, op0, op1):
+        do("v", "tensor_tensor_scan", out, a, b, init, op0, op1)
+
+    def turn32(out, a):
+        do("v", "transpose", out, a)
+
     def total_of(out, a):
         do("v", "tensor_reduce", out, a, AxisListType.X, A.add)
 
@@ -210,77 +220,101 @@ def rank_program(g, core, T, topo):
             sent[0] += share[perm[k]]
         g.remote_dma_fused(trs, local_sem=T.sem.sent)
 
-    def send_cols(ks, sem, slot, land):
+    def send_cols(ks, sem, sem2, slot, land):
         u8 = dt.uint8
         send(ks, sem, [(codes(slot, 128 * k, 128 * k + 128, u8), codes(land, 128 * rank, 128 * rank + 128, u8)) for k in ks])
-        send(ks, sem, [(plane(slot, 128 * k, 128 * k + 128), plane(land, 128 * rank, 128 * rank + 128)) for k in ks])
+        send(ks, sem2, [(plane(slot, 128 * k, 128 * k + 128), plane(land, 128 * rank, 128 * rank + 128)) for k in ks])
 
     far_ks, near_ks = list(range(len(off))), list(range(len(off), N - 1))
     all_ks = far_ks + near_ks
 
     dma("s", "lpl", v2("plb", 0, 8), ext(T.pl[:, 0:8]))
-    dma("a", "lx1", v2("xb", 512, 1024), ext(T.x[:, 512:1024]))
-    dma("s", "lx0", v2("xb", 0, 512), ext(T.x[:, 0:512]))
+    dma("a", "lx0", v2("xb", 0, 512), ext(T.x[:, 0:512]))
+    dma("s", "lx1", v2("xb", 512, 1024), ext(T.x[:, 512:1024]))
     touch("s", v2("xb", 0, 1024)[1], [])
     dma("s", "lp2", v2("p2b", 0, 8), ext(T.p2[:, 0:8]))
     dma("s", "lwv", v2("wvb", 0, 2048), ext(T.wv[:]))
     dma("s", "lw", v2("wb", 0, 512), ext(T.w[:]))
 
     iota(one("pc"), [[0, 1]], 0, 1, False)
-    iota(v2("sg1", 0, 128), [[0, 4], [2, 2], [0, 16]], -1, 0)
-    iota(v2("sg0", 0, 128), [[0, 8], [2, 2], [0, 8]], -1, 0)
-    iota(v2("vb1", 0, 128), [[32, 8], [1, 16]], -128, 0)
-    iota(v2("ctb", 0, 32), [[1, 4], [64, 8]], 0, 0)
-    iota(v2("plc", 0, 256), [[32, 4], [128, 4], [1, 16]], -256, 0)
-    iota(v2("pib", 0, 256), [[2, 4], [8, 4], [32, 16]], -256, 0)
+    iota(v2("sg1", 0, 16), [[0, 4], [2, 2], [0, 2]], -1, 0)
+    iota(v2("sg0", 0, 16), [[0, 8], [2, 2]], -1, 0)
     iota(v2("j8", 0, 128), [[0, 16], [1, 8]], 0, 0)
+    iota(v2("vb1", 0, 128), [[32, 4], [128, 2], [1, 16]], -128, 0)
+    iota(v2("ctb", 0, 32), [[1, 4], [64, 8]], 0, 0)
     iota(v2("c8", 0, 32), [[0, 4], [1, 8]], 0, 0)
     iota(v2("q16", 0, 64), [[0, 4], [1, 16]], 0, 0)
-    iota(v3("dumpc", 0, 4, 0, 4), [[64, 4], [16, 4]], 2048, 1)
-    iota(v2("io2", 0, 128), [[2, 128]], 0, 0)
     iota(v2("nadd", 0, 32), [[256, 4], [0, 8]], 1, 0)
-    iota(v2("w2t", 0, 1088), [[0, 1088]], 0, 0)
 
-    fill(v2("zt", 0, 512), 0.0)
-    for n, sh, m in (("b3", 3, 1), ("b4", 4, 1), ("bb", 3, 3)):
+    fill(v2("zt", 0, 544), 0.0)
+    fill(v2("w1t", 544, 1088), 0.0)
+    for n, sh, m in (("b3", 3, 1), ("b4", 4, 1), ("bb", 3, 3), ("j3", 0, 3), ("ji", 0, 7)):
         ts(one(n), one("pc"), sh, A.arith_shift_right, m, A.bitwise_and)
-    ts(one("thr"), one("b3"), -TINY, A.mult, TINY, A.add)
-    tt(one("bd"), one("b4"), one("b3"), A.subtract)
-    ts(one("init1"), one("bb"), 256.0, A.mult, -1.0, A.add)
+    ts(one("thrm"), one("b3"), -TINY, A.mult)
+    ts(one("out1"), one("j3"), 1.0, A.not_equal, LOW, A.mult)
+    ts(one("j0"), one("ji"), 0.0, A.is_equal)
     ts(one("h16"), one("b4"), 16.0, A.mult)
-    ts(one("bias"), one("bd"), TINY, A.mult)
-    fill(v2("zf", 0, 256), 0.0)
-    ts(v2("val1", 0, 128), v2("vb1", 0, 128), one("h16"), A.add)
+    ts(one("bias"), one("b4"), TINY, A.mult, one("thrm"), A.add)
+    ts(one("thr1"), one("out1"), one("thrm"), A.add, TINY, A.add)
+    ts(one("init1"), one("bb"), 256.0, A.mult, one("j0"), A.mult)
+    ts(v2("d0", 0, 128), v2("j8", 0, 128), 1.0, A.not_equal)
+
+    def plane_cols(tile, b, t):
+        return v2(tile, 544 * b + 28 + t, 544 * b + 540, 32)
+
+    act(v2("w1t", 0, 544), v2("zt", 0, 544), ACT.Copy)
+    act(v2("ind1", 128, 256), v2("zt", 0, 128), ACT.Copy)
+    act(v2("p1f", 0, 8), v2("plb", 0, 8), ACT.Copy)
+    for t in range(4):
+        act(plane_cols("w1t", 0, t), v2("sg0", 0, 16), ACT.Copy, scale=v2("p1f", t, t + 1))
+    act(v2("val1", 0, 128), v2("vb1", 0, 128), ACT.Identity, bias=one("h16"))
     for d in range(N):
-        fill(v2("win1", 256 * d, 256 * d + 128), 128.0)
+        act(v2("win1", 256 * d + 1, 256 * d + 129), v2("zt", 0, 128), ACT.Identity, bias=128.0)
+    for b in range(2):
+        act(v2("w2t", 544 * b, 544 * b + 544), v2("zt", 0, 544), ACT.Copy)
+    act(v2("ind2", 128, 256), v2("zt", 0, 128), ACT.Copy)
+    for t in range(4):
+        ts(plane_cols("w1t", 1, t), v2("sg1", 0, 16), v2("plb", 4 + t, 5 + t), A.mult)
+
+    quant("w1", 136, 272, "w1t", 544)
+    quant("xq", 0, 128, "xb", 0)
+    quant("xq", 128, 256, "xb", 512)
+    quant("w1", 0, 136, "w1t", 0)
     quant("xq", 256, 384, "zt", 0)
     for b in (1, 0):
-        for t in range(4):
-            ts(v2("w1t", 512 * b + t, 512 * b + 512, 4), v2("sg%d" % b, 0, 128), v2("plb", 4 * b + t, 4 * b + t + 1), A.mult)
-        if b == 1:
-            quant("w1", 128, 256, "w1t", 512)
+        for m in range(2):
+            mm(b, 128, "w1", 136 * b + 6 - 4 * m, "xq", 128 * m, m == 0, m == 1)
+    f128 = lambda n: v2(n, 0, 128)
 
-    quant("xq", 0, 256, "xb", 0)
-    quant("w1", 0, 128, "w1t", 0)
-    mm(1, 256, "w1", 128, "xq", 0)
-    mm(0, 256, "w1", 0, "xq", 0)
-    ts(v2("u1", 0, 256), v2("ps1", 0, 256), one("bias"), A.add)
-    tt(v2("mz1", 0, 256), v2("ps0", 0, 256), v2("u1", 0, 256), A.max)
-    ts(v2("ind1", 0, 256), v2("mz1", 0, 256), one("thr"), A.is_lt)
-    do("v", "tensor_tensor_scan", v2("C1", 0, 256), v2("ind1", 0, 256), v2("zf", 0, 256), one("init1"), A.add, A.add)
-    tt(v2("M1", 0, 256), v2("C1", 0, 256), v2("ind1", 0, 256), A.mult)
-    do("v", "transpose", v3("t13", 0, 8, 0, 32), v2("M1", 0, 256))
-    tt(v3("u13", 0, 8, 0, 2), v3("t13", 0, 8, 0, 16, 8), v3("t13", 0, 8, 16, 32, 8), A.add)
-    tt(v2("df1", 0, 8), v3i("u13", 0, 8, 0), v3i("u13", 0, 8, 1), A.add)
-    cp(v2("do1", 0, 8), v2("df1", 0, 8))
-    cp(by(v2("win1", 0, 1024), v2("do1", 0, 8)), v2("val1", 0, 128))
+    def places(k, n, bias, thr):
+        u, mz, ind, C, tI, tC, base, D = [s + str(k) for s in ("u", "mz", "ind", "C", "tI", "tC", "base", "D")]
+        if k == 1:
+            ts(f128(u), f128("ps1"), bias, A.add)
+        else:
+            tt(f128(u), f128("ps1"), bias, A.add)
+        tt(f128(mz), f128("ps0"), f128(u), A.max)
+        ts(f128(ind), f128(mz), thr, A.is_lt)
+        scan(v2(C, 0, 256), v2(ind, 0, 256), v2("zt", 0, 256), one("init%d" % k), A.add, A.add)
+        turn32(f128(tI), f128(ind))
+        turn32(v2(tC, 0, 256), v2(C, 0, 256))
+        scan(f128(base), f128("d0"), v2(tC, 127, 255), 0.0, A.mult, A.add)
+        st, h = 32 // n, n // 2
+        tt(v2(D, 0, 4 * n), v2(tC, 1, 128, st), v2(base, 1, 128, st), A.add)
+        tt(v3("M%d" % k, 0, 4, 0, n), v2(D, 0, 4 * n), v2(tI, 1, 128, st), A.mult)
+        tt(v3("E%d" % k, 0, 4, 0, h), v3("M%d" % k, 0, 4, 0, h), v3("M%d" % k, 0, 4, h, n), A.add)
+        tt(v3("F%d" % k, 0, 4, 0, h // 2), v3("E%d" % k, 0, 4, 0, h // 2), v3("E%d" % k, 0, 4, h // 2, h), A.add)
 
-    def lists(half, win, stride, wd, t2):
+    places(1, 8, one("bias"), one("thr1"))
+    cp(v2("do1", 0, 8), v3("F1", 0, 4, 0, 2))
+    cp(by(v2("win1", 0, 1040), v2("do1", 0, 8)), v2("val1", 0, 128))
+
+    def lists(half, win, lo, stride, wd, t2):
         a, b = 16 * half, 16 * half + 16
         for k in (2 * half, 2 * half + 1):
             for h in range(2):
-                cp(v3(wd, 8 * k, 8 * k + 8, 16 * h, 16 * h + 16), v2(win, stride * perm[k], stride * perm[k] + 128))
-        do("v", "transpose", v3(t2, a, b, 0, 32), v3(wd, a, b, 0, 32))
+                c = lo + stride * perm[k]
+                cp(v3(wd, 8 * k, 8 * k + 8, 16 * h, 16 * h + 16), v2(win, c, c + 128))
+        turn32(v3(t2, a, b, 0, 32), v3(wd, a, b, 0, 32))
 
     def pick(dst, a, b, src, w, offs, k):
         o = v2(offs, 8 * k, 8 * k + (b - a) // 16)
@@ -289,26 +323,29 @@ def rank_program(g, core, T, topo):
 
     for half in range(2):
         a, b = 16 * half, 16 * half + 16
-        lists(half, "win1", 256, "wd1", "t21")
+        lists(half, "win1", 1, 256, "wd1", "t21")
         tt(v2("l1", a, b), v3i("t21", a, b, 0), v3i("t21", a, b, 16), A.add)
         cp(v2("off1", a, b), v2("l1", a, b))
         if half == 0:
             pick("slota", 0, 256, "xq", 384, "off1", 0)
         else:
             pick("slota", 256, 384, "xq", 384, "off1", 2)
-        send_cols(far_ks if half == 0 else near_ks, "c1", "slota", "landa")
+        send_cols(far_ks if half == 0 else near_ks, "c1", "c1", "slota", "landa")
     send(all_ks, "n1", [(v2("off1", 8 * k, 8 * k + 8), v2("nl", 8 * rank, 8 * rank + 8)) for k in all_ks])
     pick("landa", 128 * rank, 128 * rank + 128, "xq", 384, "off1", 3)
     cp(v2("nl", 8 * rank, 8 * rank + 8), v2("off1", 24, 32))
 
+    iota(v2("plc", 0, 256), [[32, 4], [128, 4], [1, 16]], -256, 0)
+    iota(v2("pib", 0, 256), [[2, 4], [8, 4], [32, 16]], -256, 0)
+    iota(v2("io2", 0, 128), [[2, 128]], 0, 0)
+    iota(v3("dumpc", 0, 4, 0, 4), [[64, 4], [16, 4]], 0, 1)
     for d in range(N):
-        iota(v2("win2", 512 * d, 512 * d + 128), [[0, 128]], 256, 0)
+        iota(v2("win2", 512 * d + DUMP + 1, 512 * d + DUMP + 129), [[0, 128]], 256, 0)
     act(v2("p2f", 0, 8), v2("p2b", 0, 8), ACT.Copy)
     for b in range(2):
         for t in range(4):
-            act(v2("w2t", 544 * b + 28 + t, 544 * b + 540, 32), v2("sg%d" % b, 0, 128, 8), ACT.Copy,
-                scale=v2("p2f", 4 * b + t, 4 * b + t + 1))
-    for n, sh, m in (("qi", 0, 15), ("gi", 4, 7), ("oi", 0, 1), ("ji", 0, 7)):
+            act(plane_cols("w2t", b, t), v2("sg%d" % b, 0, 16), ACT.Copy, scale=v2("p2f", 4 * b + t, 4 * b + t + 1))
+    for n, sh, m in (("qi", 0, 15), ("gi", 4, 7), ("oi", 0, 1)):
         ts(one(n), one("pc"), sh, A.arith_shift_right, m, A.bitwise_and)
     ts(one("q4"), one("qi"), 4.0, A.mult)
     ts(one("evf"), one("oi"), -1.0, A.mult, 1.0, A.add)
@@ -320,19 +357,23 @@ def rank_program(g, core, T, topo):
     act(v2("va", 0, 256), v2("plc", 0, 256), ACT.Identity, bias=one("hc"), scale=one("evf"))
     act(v2("vp", 0, 256), v2("pib", 0, 256), ACT.Copy, scale=one("oddf"))
     quant("wvq", 0, 512, "wvb", 0)
-    ts(one("t512"), one("bb"), 512.0, A.mult, -1.0, A.add)
-    ts(one("j0"), one("ji"), 0.0, A.is_equal)
+    quant("w2", 0, 136, "w2t", 0)
+    quant("w2", 136, 272, "w2t", 544)
+    ts(one("out2"), one("evf"), LOW, A.mult)
+    ts(one("kk"), one("bb"), 512.0, A.mult, float(DUMP), A.add)
     cp(one("qf"), one("qi"))
     cp(one("gf"), one("gi"))
-    tt(one("init2"), one("t512"), one("j0"), A.mult)
+    ts(one("thr2"), one("out2"), one("thrm"), A.add, TINY, A.add)
+    tt(one("init2"), one("kk"), one("j0"), A.mult)
     fill(v2("X", 0, 32), 0.0)
     fill(v2("X", 9, 32, 2), 8.0)
     fill(v2("tabrow", 512, 520), 0.0)
     fill(v2("idp", 0, 32), 0.0)
     quant("hq", 512, 640, "zt", 0)
-    ts(v2("d0", 0, 128), v2("j8", 0, 128), 1.0, A.not_equal)
     ts(v2("dm1", 0, 32), v2("c8", 0, 32), one("gf"), A.is_equal)
     ts(v2("dm2", 0, 64), v2("q16", 0, 64), one("qf"), A.is_equal)
+    ts(v2("f8", 0, 32), v2("c8", 0, 32), 0.0, A.not_equal)
+    ts(v2("f16", 0, 64), v2("q16", 0, 64), 0.0, A.not_equal)
     tt(v2("val2", 0, 256), v2("va", 0, 256), v2("vp", 0, 256), A.add)
 
     for s in range(N):
@@ -341,113 +382,100 @@ def rank_program(g, core, T, topo):
             arrive("n1", every, v2("nl", 8 * s, 8 * s + 8))
     for t in range(4):
         pick("ct", 128 * t, 128 * t + 128, "landa", 512, "offct", t)
-    quant("w2", 0, 136, "w2t", 0)
-    quant("w2", 136, 272, "w2t", 544)
+
+    def empty(q, tile, lo, t, bank, n, f):
+        o, z = v2(tile, lo + t, lo + 4 * n, 4), v2("ps%d" % bank, 0, n)
+        if f == "copy":
+            act(o, z, ACT.Copy) if q == "a" else cp(o, z)
+        elif f == "relu":
+            act(o, z, ACT.Relu, scale=0.0625) if q == "a" else ts(o, z, 0.0, A.max, 0.0625, A.mult)
+        else:
+            act(o, z, ACT.Copy, scale=0.0625) if q == "a" else ts(o, z, 0.0625, A.mult)
+
     for t in range(4):
         mm(t, 512, "ct", 128 * t, "wvq", 0)
-        o, z = v2("vt", t, 2048, 4), v2("ps%d" % t, 0, 512)
-        if t % 2 == 0:
-            act(o, z, ACT.Copy)
-        else:
-            cp(o, z)
+        empty("avav"[t], "vt", 0, t, t, 512, "copy")
         if t == 1:
             ts(v2("fF", 0, 32), v2("nl", 0, 32), 255.5, A.is_lt)
+            cp(v2("nf", 0, 32), v2("nl", 0, 32))
             for m in range(4):
                 total_of(v2("X", 1 + 2 * m, 2 + 2 * m), v2("fF", 8 * m, 8 * m + 8))
+            tt(v2("nt", 0, 32), v2("nf", 0, 32), v2("nadd", 0, 32), A.add)
+    dma("s", "ltb", (T.tabrow[0:1, 0:512], v2("tabrow", 0, 512)[1], []), (T.nt[0:16, 0:32], v2("nt", 0, 32)[1], []))
+    do("g", "partition_broadcast", v2("tab", 0, 520), (T.tabrow[0:1, 0:520], v2("tabrow", 0, 520)[1], []), 128)
     quant("vq", 0, 512, "vt", 0)
-    for h in range(2):
+    for h, who in enumerate(("aaaa", "aaav")):
         for t in range(4):
             bank = 4 * (1 - h) + t
             mm(bank, 256, "ct", 128 * t, "landa", 256 * h)
-            o, z = v2("at", 1024 * h + t, 1024 * h + 1024, 4), v2("ps%d" % bank, 0, 256)
-            if t == 3 or (h == 1 and t == 1):
-                ts(o, z, 0.0, A.max, 0.0625, A.mult)
-            else:
-                act(o, z, ACT.Relu, scale=0.0625)
+            empty(who[t], "at", 1024 * h, t, bank, 256, "relu")
         quant("aq", 256 * h, 256 * h + 256, "at", 1024 * h)
-    do("v", "transpose", v2("xt", 0, 32), v2("X", 0, 32))
-    total_of(one("cnt2"), v2("xt", 0, 32))
-    for h in range(2):
+    for lo, n, b0, who in ((0, 256, 4, "aava"), (256, 128, 0, "aava"), (384, 128, 4, "avav")):
         for i in range(4):
-            bank = 4 * (1 - h) + i
-            mm(bank, 256, "vq", 128 * i, "aq", 256 * h)
-            o, z = v2("ht", 1024 * h + i, 1024 * h + 1024, 4), v2("ps%d" % bank, 0, 256)
-            if i % 2 == 0:
-                act(o, z, ACT.Copy, scale=0.0625)
-            else:
-                ts(o, z, 0.0625, A.mult)
-        quant("hq", 256 * h, 256 * h + 256, "ht", 1024 * h)
-    for h in range(2):
-        for b in (1, 0):
-            for m in (2 * h, 2 * h + 1):
-                mm(4 + b, 128, "w2", 136 * b + 6 - 2 * m, "hq", 128 * m, m == 0, m == 3)
+            mm(b0 + i, n, "vq", 128 * i, "aq", lo)
+        if lo == 384:
+            for b in (1, 0):
+                for m in range(3):
+                    mm(b, 128, "w2", 136 * b + 6 - 2 * m, "hq", 128 * m, m == 0, False)
+        for i in range(4):
+            empty(who[i], "ht", 4 * lo, i, b0 + i, n, "scale")
+        if lo == 0:
+            turn32(v2("xt", 0, 32), v2("X", 0, 32))
+            total_of(one("cnt2"), v2("xt", 0, 32))
+        quant("hq", lo, lo + n, "ht", 4 * lo)
+    for b in (1, 0):
+        mm(b, 128, "w2", 136 * b, "hq", 384, False, True)
 
-    f128 = lambda n: v2(n, 0, 128)
-    ts(f128("te"), f128("io2"), one("cnt2"), A.is_ge, LOW, A.mult)
-    ts(f128("thrm"), f128("te"), one("thr"), A.add)
-    cp(v2("nf", 0, 32), v2("nl", 0, 32))
-    tt(v2("nt", 0, 32), v2("nf", 0, 32), v2("nadd", 0, 32), A.add)
-    dma("s", "ltb", (T.tabrow[0:1, 0:512], v2("tabrow", 0, 512)[1], []), (T.nt[0:16, 0:32], v2("nt", 0, 32)[1], []))
-    do("g", "partition_broadcast", v2("tab", 0, 520), (T.tabrow[0:1, 0:520], v2("tabrow", 0, 520)[1], []), 128)
-    ts(f128("u2"), f128("ps5"), one("bias"), A.add)
-    tt(f128("mz2"), f128("ps4"), f128("u2"), A.max)
-    tt(f128("ind2"), f128("mz2"), f128("thrm"), A.is_lt)
-    do("v", "tensor_tensor_scan", f128("C2"), f128("ind2"), f128("zf"), one("init2"), A.add, A.add)
-    act(v2("mb", 128, 256), f128("zf"), ACT.Identity, bias=v2("C2", 127, 128))
-    ts(f128("pen"), f128("ind2"), -FAR, A.mult, FAR, A.add)
-    tt(f128("mb"), f128("C2"), f128("pen"), A.add)
-    do("v", "transpose", v2("tt", 0, 256), v2("mb", 0, 256))
-    do("v", "tensor_tensor_scan", f128("base"), f128("d0"), v2("tt", 127, 255), 0.0, A.mult, A.add)
-    tt(v3("D3", 0, 4, 0, 32), f128("tt"), f128("base"), A.add)
-    tt(v3("E3", 0, 4, 0, 16), v3("D3", 0, 4, 0, 16), v3("D3", 0, 4, 16, 32), A.min)
-    tt(v3("F3", 0, 4, 0, 8), v3("E3", 0, 4, 0, 8), v3("E3", 0, 4, 8, 16), A.min)
-    tt(v3("dst3", 0, 4, 0, 4), v3("F3", 0, 4, 1, 8, 2), v3("dumpc", 0, 4, 0, 4), A.min)
-    cp(v2("do2", 0, 16), v3("dst3", 0, 4, 0, 4))
-    cp(by(v2("win2", 0, 2432), v2("do2", 0, 16)), v2("val2", 0, 256))
+    ts(f128("te"), f128("io2"), one("cnt2"), A.is_ge, HIGH, A.mult)
+    ts(f128("bm"), f128("te"), one("bias"), A.add)
+    places(2, 16, f128("bm"), one("thr2"))
+    tt(v3("dst2", 0, 4, 0, 4), v3("F2", 0, 4, 0, 4), v3("dumpc", 0, 4, 0, 4), A.max)
+    cp(v2("do2", 0, 16), v3("dst2", 0, 4, 0, 4))
+    cp(by(v2("win2", 0, 2448), v2("do2", 0, 16)), v2("val2", 0, 256))
     for half in range(2):
         a, b = 16 * half, 16 * half + 16
-        lists(half, "win2", 512, "wd2", "t22")
+        lists(half, "win2", DUMP + 1, 512, "wd2", "t22")
         tt(v3("l2", a, b, 0, 2), v3("t22", a, b, 0, 2), v3("t22", a, b, 16, 18), A.add)
         cp(v2("off2", a, b), v3i("l2", a, b, 0))
         if half == 0:
             pick("slotb", 0, 256, "hq", 640, "off2", 0)
         else:
             pick("slotb", 256, 384, "hq", 640, "off2", 2)
-        send_cols(far_ks if half == 0 else near_ks, "c2_%d" % rank, "slotb", "landb")
+        send_cols(far_ks if half == 0 else near_ks, "c2_%d" % rank, "s2_%d" % rank, "slotb", "landb")
     tt(v2("pd", 0, 32), v3i("l2", 0, 32, 1), v2("dm1", 0, 32), A.mult)
-    for k in range(4):
-        total_of(v2("pdr", k, k + 1), v2("pd", 8 * k, 8 * k + 8))
-    cp(v2("offD", 0, 4), v2("pdr", 0, 4))
+    scan(v2("pds", 0, 32), v2("f8", 0, 32), v2("pd", 0, 32), 0.0, A.mult, A.add)
+    cp(v2("offD", 0, 4), v2("pds", 7, 32, 8))
     cp(v2("ga", 0, 64), by(v2("tab", 0, 520), v2("offD", 0, 4)))
     tt(v2("gm", 0, 64), v2("ga", 0, 64), v2("dm2", 0, 64), A.mult)
-    for k in range(4):
-        total_of(v2("idr", k, k + 1), v2("gm", 16 * k, 16 * k + 16))
-    cp(v2("idu", 0, 4), v2("idr", 0, 4))
+    scan(v2("gms", 0, 64), v2("f16", 0, 64), v2("gm", 0, 64), 0.0, A.mult, A.add)
+    cp(v2("idu", 0, 4), v2("gms", 15, 64, 16))
     send(all_ks, "n2", [(v2("idu", k, k + 1), v2("idl", 8 * rank, 8 * rank + 1)) for k in all_ks])
     pick("landb", 128 * rank, 128 * rank + 128, "hq", 640, "off2", 3)
-    cp(v2("idl", 8 * rank, 8 * rank + 1), v2("idr", 3, 4))
+    cp(v2("idl", 8 * rank, 8 * rank + 1), v2("idu", 3, 4))
     quant("wq", 0, 128, "wb", 0)
 
     for s in range(N):
         if s != rank:
-            arrive("c2_%d" % s, 2 * share[s], codes("landb", 128 * s, 128 * s + 128), plane("landb", 128 * s, 128 * s + 128))
+            arrive("c2_%d" % s, share[s], codes("landb", 128 * s, 128 * s + 128))
+            arrive("s2_%d" % s, share[s], plane("landb", 128 * s, 128 * s + 128))
             arrive("n2", every, v2("idl", 8 * s, 8 * s + 1))
     turn = [rank] + near + off
+    for s in turn:
+        dma("s", "oc%d" % s, ext(T.oc[:, 512 * s:512 * s + 512]), codes("landb", 128 * s, 128 * s + 128, dt.uint8))
     for i, s in enumerate(turn):
-        bank = (6, 7, 0, 1)[i]
+        bank = (6, 7, 2, 3)[i]
         mm(bank, 128, "wq", 0, "landb", 128 * s)
         o, z = v2("yb", 128 * s, 128 * s + 128), v2("ps%d" % bank, 0, 128)
         if i < 3:
             act(o, z, ACT.Copy)
         else:
             cp(o, z)
-        dma("s", "oc%d" % s, ext(T.oc[:, 512 * s:512 * s + 512]), codes("landb", 128 * s, 128 * s + 128, dt.uint8))
         dma("a" if i < 3 else "s", "yy%d" % s, ext(T.y[:, 128 * s:128 * s + 128]), o)
     for k in range(4):
         dma("a" if k % 2 else "s", "os%d" % k, ext(T.osc[4 * k:4 * k + 4, :]),
             (T.landbs[32 * k:32 * k + 4, 0:512], plane("landb", 0, 512)[1], []))
     ts(v2("idp", 0, 4), v2("idl", 0, 32, 8), -1.0, A.add)
-    do("v", "transpose", v2("idt", 0, 32), v2("idp", 0, 32))
+    turn32(v2("idt", 0, 32), v2("idp", 0, 32))
     for s in range(N):
         dma("a" if s % 2 else "s", "ii%d" % s, ext(T["id"][0:1, 128 * s:128 * s + 128]),
             (T.idt[s:128:32, 0:32], v2("idt", 0, 32)[1], []))

@@ -3,35 +3,31 @@ from concourse.mybir import dt, AluOpType, AxisListType, ActivationFunctionType
 
 F, B, I, U = "float32", "bfloat16", "int32", "uint16"
 Q, S8 = "float8_e4m3fn_x4", "uint8"
-COL = {n: ("ki", k) for k, n in enumerate(("pc", "b3", "b4", "bb", "j3", "ji", "qi", "gi", "oi"))}
-COL.update({n: ("kf", k) for k, n in enumerate((
-    "thrm", "bias", "h16", "j0", "init1", "init2", "out1", "out2", "thr1", "thr2", "q4", "qf", "gf", "oddf", "evf",
-    "t15", "hc", "cnt2", "kk"))})
+COL = {n: ("ki", k) for k, n in enumerate(("pc", "b2", "b3", "b4", "qi", "gi"))}
+COL.update({n: ("kf", k) for k, n in enumerate(("t0a", "t1a", "t0b", "h16", "q4", "gf", "cnt0", "cnt1"))})
 SCRATCH = {}
 for _n, _w, _t in (
         ("plb", 8, B), ("p2b", 8, B), ("p1f", 8, F), ("p2f", 8, F), ("xb", 1024, B), ("wvb", 2048, B), ("wb", 512, B),
-        ("w1t", 1088, B), ("zt", 544, B), ("w2t", 1088, B), ("at", 2048, B), ("vt", 2048, B), ("ht", 2048, B),
-        ("sg0", 16, B), ("sg1", 16, B), ("val1", 128, B), ("val2", 256, B), ("win1", 1040, B), ("win2", 2448, B),
-        ("ki", 16, I), ("kf", 24, F),
-        ("vb1", 128, F), ("ctb", 32, F), ("ctf", 32, F), ("j8", 128, B), ("d0", 128, B), ("plc", 256, F), ("pib", 256, F),
-        ("va", 256, F), ("vp", 256, F), ("c8", 32, F), ("dm1", 32, F), ("f8", 32, F), ("q16", 64, F), ("dm2", 64, F),
-        ("f16", 64, F), ("io2", 128, F), ("nadd", 32, F), ("X", 32, F), ("xt", 32, F), ("fF", 32, F), ("nf", 32, F),
-        ("nt", 32, F), ("te", 128, F), ("bm", 128, F), ("tabrow", 520, F), ("tab", 520, F),
-        ("u1", 128, F), ("mz1", 128, F), ("ind1", 256, B), ("C1", 256, B), ("tI1", 128, B), ("tC1", 256, B),
-        ("base1", 128, F), ("D1", 32, F), ("l1", 32, F),
-        ("u2", 128, F), ("mz2", 128, F), ("ind2", 256, B), ("C2", 256, B), ("tI2", 128, B), ("tC2", 256, B),
-        ("base2", 128, F), ("D2", 64, F),
+        ("w1t", 1024, B), ("zt", 576, B), ("w2t", 1152, B), ("at", 2048, B), ("vt", 2048, B), ("ht", 2048, B),
+        ("sa0", 16, B), ("sa1", 16, B), ("sb0", 32, B), ("sb1", 32, B), ("hm", 32, B),
+        ("val1", 128, B), ("val2", 256, B), ("win1", 1040, B), ("win2", 2320, B), ("ki", 16, I), ("kf", 24, F),
+        ("vb1", 128, F), ("ctb", 32, F), ("plc", 256, F), ("c8", 32, F), ("dm1", 32, F), ("f8", 32, F), ("q16", 64, F),
+        ("dm2", 64, F), ("f16", 64, F), ("io2", 128, B), ("nadd", 32, F), ("X", 64, F), ("xt", 64, F), ("fF", 32, F),
+        ("nf", 32, F), ("nt", 32, F), ("ntt", 32, F), ("tb2", 256, B), ("am", 288, B), ("a1", 32, F), ("a2", 64, F),
+        ("c64", 16, F), ("dmp", 16, F), ("tabrow", 520, F), ("tab", 520, F),
+        ("g1", 256, B), ("ind1", 256, B), ("C1", 256, B), ("tI1", 256, B), ("tC1", 256, B), ("M1", 32, F), ("R1", 32, F),
+        ("l1", 32, F), ("l2", 32, F),
+        ("g2", 256, B), ("ind2", 416, B), ("C2", 416, B), ("J2", 256, B), ("tJ2", 256, B), ("tC2", 416, B), ("D2", 64, F),
+        ("M2", 64, F), ("R2", 64, F), ("dst2", 16, F),
         ("pd", 32, F), ("pds", 32, F), ("ga", 64, F), ("gm", 64, F), ("gms", 64, F), ("idp", 32, F),
         ("idt", 32, F), ("yb", 512, F),
         ("do1", 8, U), ("do2", 16, U), ("off1", 32, U), ("off2", 32, U), ("offct", 32, U), ("offD", 4, U), ("nl", 32, U),
         ("idu", 4, U), ("idl", 32, U)):
     SCRATCH[_n] = ("sbuf", [128, _w], _t)
-for _n, _a, _b, _t in (("M1", 4, 8, F), ("E1", 4, 4, F), ("F1", 4, 2, F), ("wd1", 32, 32, B), ("t21", 32, 32, B),
-                       ("M2", 4, 16, F), ("E2", 4, 8, F), ("F2", 4, 4, F), ("dst2", 4, 4, F), ("dumpc", 4, 4, F),
-                       ("wd2", 32, 32, B), ("t22", 32, 32, B), ("l2", 32, 2, F)):
-    SCRATCH[_n] = ("sbuf", [128, _a, _b], _t)
-for _n, _w in (("w1", 272), ("xq", 384), ("slota", 384), ("landa", 512), ("ct", 512), ("wvq", 512), ("aq", 512), ("vq", 512),
-               ("w2", 272), ("hq", 640), ("slotb", 384), ("landb", 512), ("wq", 128)):
+for _n in ("wd1", "t21", "wd2", "t22"):
+    SCRATCH[_n] = ("sbuf", [128, 32, 32], B)
+for _n, _w in (("w1", 256), ("xq", 384), ("slota", 384), ("landa", 512), ("ct", 512), ("wvq", 512), ("aq", 512), ("vq", 512),
+               ("w2", 288), ("hq", 640), ("slotb", 384), ("landb", 512), ("wq", 128)):
     SCRATCH[_n + "c"] = ("sbuf", [128, _w], Q)
     SCRATCH[_n + "s"] = ("sbuf", [128, _w], S8)
 for _k in range(8):
@@ -42,8 +38,8 @@ SEMAPHORES = (["sv", "sa", "sp", "sg", "sent", "c1", "n1", "n2", "lpl", "lx0", "
               + ["%s%d" % (n, k) for n in ("oc", "os", "yy", "ii") for k in range(4)])
 
 TINY = 2.0 ** -120
-LOW, HIGH = -2.0 ** 99, 2.0 ** 99
-DUMP = 384
+LOW, FAR = -2.0 ** 99, 2.0 ** 20
+LIST1, LIST2 = 4, 260
 
 
 def rank_program(g, core, T, topo):
@@ -97,13 +93,15 @@ def rank_program(g, core, T, topo):
     def v2(name, a, b, step=1):
         return (T[name][:, a:b:step] if step > 1 else T[name][:, a:b], [(name, a, b, step, 1)], [])
 
+    def half(name, h):
+        return v2(name, 128 * h, 128 * h + 128)
+
     def one(n):
         return v2(COL[n][0], COL[n][1], COL[n][1] + 1)
 
-    def v3(name, a, b, c, d, step=1):
+    def v3(name, a, b, c, d):
         w = SCRATCH[name][1][2]
-        return (T[name][:, a:b, c:d:step] if step > 1 else T[name][:, a:b, c:d],
-                [(name, a * w + c, (b - 1) * w + d, w, d - c)], [])
+        return (T[name][:, a:b, c:d], [(name, a * w + c, (b - 1) * w + d, w, d - c)], [])
 
     def v3i(name, a, b, c):
         w = SCRATCH[name][1][2]
@@ -237,144 +235,145 @@ def rank_program(g, core, T, topo):
     dma("s", "lw", v2("wb", 0, 512), ext(T.w[:]))
 
     iota(one("pc"), [[0, 1]], 0, 1, False)
-    iota(v2("sg1", 0, 16), [[0, 4], [2, 2], [0, 2]], -1, 0)
-    iota(v2("sg0", 0, 16), [[0, 8], [2, 2]], -1, 0)
-    iota(v2("j8", 0, 128), [[0, 16], [1, 8]], 0, 0)
-    iota(v2("vb1", 0, 128), [[32, 4], [128, 2], [1, 16]], -128, 0)
+    iota(v2("sa1", 0, 16), [[0, 4], [-2, 2], [0, 2]], 1, 0)
+    iota(v2("sa0", 0, 16), [[0, 8], [-2, 2]], 1, 0)
+    iota(v2("vb1", 0, 128), [[32, 8], [1, 16]], -128, 0)
     iota(v2("ctb", 0, 32), [[1, 4], [64, 8]], 0, 0)
     iota(v2("c8", 0, 32), [[0, 4], [1, 8]], 0, 0)
-    iota(v2("q16", 0, 64), [[0, 4], [1, 16]], 0, 0)
+    iota(v2("q16", 0, 64), [[0, 4], [4, 16]], 0, 0)
     iota(v2("nadd", 0, 32), [[256, 4], [0, 8]], 1, 0)
+    iota(v2("sb0", 0, 32), [[0, 16], [-2, 2]], 1, 0)
+    iota(v2("sb1", 0, 32), [[0, 8], [-2, 2], [0, 2]], 1, 0)
+    iota(v2("hm", 0, 32), [[0, 4], [-1, 2], [0, 4]], 1, 0)
+    iota(v2("c64", 0, 16), [[64, 16]], -1024, 0)
 
-    fill(v2("zt", 0, 544), 0.0)
-    fill(v2("w1t", 544, 1088), 0.0)
-    for n, sh, m in (("b3", 3, 1), ("b4", 4, 1), ("bb", 3, 3), ("j3", 0, 3), ("ji", 0, 7)):
-        ts(one(n), one("pc"), sh, A.arith_shift_right, m, A.bitwise_and)
-    ts(one("thrm"), one("b3"), -TINY, A.mult)
-    ts(one("out1"), one("j3"), 1.0, A.not_equal, LOW, A.mult)
-    ts(one("j0"), one("ji"), 0.0, A.is_equal)
+    fill(v2("zt", 0, 576), 0.0)
+    fill(v2("w1t", 512, 1024), 0.0)
+    for n, sh in (("b4", 4), ("b3", 3)):
+        ts(one(n), one("pc"), sh, A.arith_shift_right, 1, A.bitwise_and)
+    ts(one("t1a"), one("b4"), TINY, A.mult)
+    ts(one("t0a"), one("b3"), TINY, A.mult)
     ts(one("h16"), one("b4"), 16.0, A.mult)
-    ts(one("bias"), one("b4"), TINY, A.mult, one("thrm"), A.add)
-    ts(one("thr1"), one("out1"), one("thrm"), A.add, TINY, A.add)
-    ts(one("init1"), one("bb"), 256.0, A.mult, one("j0"), A.mult)
-    ts(v2("d0", 0, 128), v2("j8", 0, 128), 1.0, A.not_equal)
+    quant("xq", 256, 384, "zt", 0)
+    fill(v2("a1", 0, 32), 0.25)
+    fill(v2("a1", 0, 32, 4), LOW)
 
-    def plane_cols(tile, b, t):
-        return v2(tile, 544 * b + 28 + t, 544 * b + 540, 32)
+    def plane_cols(k, b, t):
+        return v2("w1t", 512 * b + t, 512 * b + 512, 32) if k == 1 else v2("w2t", 576 * b + 64 + t, 576 * b + 564, 16)
 
-    act(v2("w1t", 0, 544), v2("zt", 0, 544), ACT.Copy)
-    act(v2("ind1", 128, 256), v2("zt", 0, 128), ACT.Copy)
+    act(v2("w1t", 0, 512), v2("zt", 0, 512), ACT.Copy)
     act(v2("p1f", 0, 8), v2("plb", 0, 8), ACT.Copy)
     for t in range(4):
-        act(plane_cols("w1t", 0, t), v2("sg0", 0, 16), ACT.Copy, scale=v2("p1f", t, t + 1))
+        act(plane_cols(1, 0, t), v2("sa0", 0, 16), ACT.Copy, scale=v2("p1f", t, t + 1))
     act(v2("val1", 0, 128), v2("vb1", 0, 128), ACT.Identity, bias=one("h16"))
-    for d in range(N):
-        act(v2("win1", 256 * d + 1, 256 * d + 129), v2("zt", 0, 128), ACT.Identity, bias=128.0)
+    act(v2("win1", LIST1, LIST1 + 516), v2("zt", 0, 516), ACT.Identity, bias=128.0)
     for b in range(2):
-        act(v2("w2t", 544 * b, 544 * b + 544), v2("zt", 0, 544), ACT.Copy)
-    act(v2("ind2", 128, 256), v2("zt", 0, 128), ACT.Copy)
+        act(v2("w2t", 576 * b, 576 * b + 576), v2("zt", 0, 576), ACT.Copy)
+    act(v2("ind2", 256, 416), v2("zt", 0, 160), ACT.Copy)
+    act(v2("am", 0, 288), v2("zt", 0, 288), ACT.Identity, bias=1.0)
+    act(v2("a2", 0, 64), v2("zt", 0, 64), ACT.Identity, bias=0.25)
     for t in range(4):
-        ts(plane_cols("w1t", 1, t), v2("sg1", 0, 16), v2("plb", 4 + t, 5 + t), A.mult)
+        ts(plane_cols(1, 1, t), v2("sa1", 0, 16), v2("plb", 4 + t, 5 + t), A.mult)
 
-    quant("w1", 136, 272, "w1t", 544)
+    quant("w1", 128, 256, "w1t", 512)
     quant("xq", 0, 128, "xb", 0)
+    quant("w1", 0, 128, "w1t", 0)
     quant("xq", 128, 256, "xb", 512)
-    quant("w1", 0, 136, "w1t", 0)
-    quant("xq", 256, 384, "zt", 0)
-    for b in (1, 0):
-        for m in range(2):
-            mm(b, 128, "w1", 136 * b + 6 - 4 * m, "xq", 128 * m, m == 0, m == 1)
-    f128 = lambda n: v2(n, 0, 128)
+    for h in range(2):
+        for b in (1, 0):
+            mm(2 * h + b, 128, "w1", 128 * b, "xq", 128 * h)
+    prod = lambda h, b: v2("ps%d" % (2 * h + b), 0, 128)
 
-    def places(k, n, bias, thr):
-        u, mz, ind, C, tI, tC, base, D = [s + str(k) for s in ("u", "mz", "ind", "C", "tI", "tC", "base", "D")]
+    def gate(k, h):
+        o = half("g%d" % k, h)
         if k == 1:
-            ts(f128(u), f128("ps1"), bias, A.add)
+            ts(o, prod(h, 1), one("t1a"), A.is_ge, LOW, A.mult)
+            ts(o, o, one("t0a"), A.add)
         else:
-            tt(f128(u), f128("ps1"), bias, A.add)
-        tt(f128(mz), f128("ps0"), f128(u), A.max)
-        ts(f128(ind), f128(mz), thr, A.is_lt)
-        scan(v2(C, 0, 256), v2(ind, 0, 256), v2("zt", 0, 256), one("init%d" % k), A.add, A.add)
-        turn32(f128(tI), f128(ind))
-        turn32(v2(tC, 0, 256), v2(C, 0, 256))
-        scan(f128(base), f128("d0"), v2(tC, 127, 255), 0.0, A.mult, A.add)
-        st, h = 32 // n, n // 2
-        tt(v2(D, 0, 4 * n), v2(tC, 1, 128, st), v2(base, 1, 128, st), A.add)
-        tt(v3("M%d" % k, 0, 4, 0, n), v2(D, 0, 4 * n), v2(tI, 1, 128, st), A.mult)
-        tt(v3("E%d" % k, 0, 4, 0, h), v3("M%d" % k, 0, 4, 0, h), v3("M%d" % k, 0, 4, h, n), A.add)
-        tt(v3("F%d" % k, 0, 4, 0, h // 2), v3("E%d" % k, 0, 4, 0, h // 2), v3("E%d" % k, 0, 4, h // 2, h), A.add)
+            tt(o, prod(h, 1), half("tb2", h), A.is_ge)
+            ts(o, o, LOW, A.mult, one("t0b"), A.add)
 
-    places(1, 8, one("bias"), one("thr1"))
-    cp(v2("do1", 0, 8), v3("F1", 0, 4, 0, 2))
+    def member(k, h):
+        tt(half("ind%d" % k, h), prod(h, 0), half("g%d" % k, h), A.is_lt)
+
+    def count1(h):
+        scan(half("C1", h), half("ind1", h), v2("zt", 0, 128), v2("C1", 127, 128) if h else 0.0, A.add, A.add)
+
+    gate(1, 0)
+    member(1, 0)
+    gate(1, 1)
+    count1(0)
+    member(1, 1)
+    turn32(half("tI1", 0), half("ind1", 0))
+    count1(1)
+    turn32(half("tC1", 0), half("C1", 0))
+    turn32(half("tI1", 1), half("ind1", 1))
+    turn32(half("tC1", 1), half("C1", 1))
+    tt(v2("M1", 0, 32), v2("tI1", 0, 256, 8), v2("tC1", 0, 256, 8), A.mult)
+    scan(v2("R1", 0, 32), v2("a1", 0, 32), v2("M1", 0, 32), 0.0, A.add, A.max)
+    ts(v2("do1", 0, 8), v2("R1", 3, 32, 4), 4.0, A.mult)
     cp(by(v2("win1", 0, 1040), v2("do1", 0, 8)), v2("val1", 0, 128))
 
-    def lists(half, win, lo, stride, wd, t2):
-        a, b = 16 * half, 16 * half + 16
-        for k in (2 * half, 2 * half + 1):
+    def spread(win, lo, wd):
+        for k in range(4):
             for h in range(2):
-                c = lo + stride * perm[k]
-                cp(v3(wd, 8 * k, 8 * k + 8, 16 * h, 16 * h + 16), v2(win, c, c + 128))
-        turn32(v3(t2, a, b, 0, 32), v3(wd, a, b, 0, 32))
+                o, z = v3(wd, 8 * k, 8 * k + 8, 16 * h, 16 * h + 16), v2(win, lo + perm[k], lo + perm[k] + 509, 4)
+                if k > 1 or k + h == 0:
+                    act(o, z, ACT.Copy)
+                else:
+                    cp(o, z)
 
     def pick(dst, a, b, src, w, offs, k):
         o = v2(offs, 8 * k, 8 * k + (b - a) // 16)
         cp(codes(dst, a, b, dt.uint32), by(codes(src, 0, w, dt.uint32), o))
         act(plane(dst, a, b), by(plane(src, 0, w), o), ACT.Copy)
 
-    for half in range(2):
-        a, b = 16 * half, 16 * half + 16
-        lists(half, "win1", 1, 256, "wd1", "t21")
+    spread("win1", LIST1, "wd1")
+    for hf in range(2):
+        a, b = 16 * hf, 16 * hf + 16
+        turn32(v3("t21", a, b, 0, 32), v3("wd1", a, b, 0, 32))
         tt(v2("l1", a, b), v3i("t21", a, b, 0), v3i("t21", a, b, 16), A.add)
         cp(v2("off1", a, b), v2("l1", a, b))
-        if half == 0:
+        if hf == 0:
             pick("slota", 0, 256, "xq", 384, "off1", 0)
         else:
             pick("slota", 256, 384, "xq", 384, "off1", 2)
-        send_cols(far_ks if half == 0 else near_ks, "c1", "c1", "slota", "landa")
+        send_cols(far_ks if hf == 0 else near_ks, "c1", "c1", "slota", "landa")
     send(all_ks, "n1", [(v2("off1", 8 * k, 8 * k + 8), v2("nl", 8 * rank, 8 * rank + 8)) for k in all_ks])
     pick("landa", 128 * rank, 128 * rank + 128, "xq", 384, "off1", 3)
     cp(v2("nl", 8 * rank, 8 * rank + 8), v2("off1", 24, 32))
 
-    iota(v2("plc", 0, 256), [[32, 4], [128, 4], [1, 16]], -256, 0)
-    iota(v2("pib", 0, 256), [[2, 4], [8, 4], [32, 16]], -256, 0)
+    for h in range(2):
+        iota(half("plc", h), [[32, 4], [256, 2], [1, 16]], 128 * h - 256, 0)
     iota(v2("io2", 0, 128), [[2, 128]], 0, 0)
-    iota(v3("dumpc", 0, 4, 0, 4), [[64, 4], [16, 4]], 0, 1)
-    for d in range(N):
-        iota(v2("win2", 512 * d + DUMP + 1, 512 * d + DUMP + 129), [[0, 128]], 256, 0)
+    iota(v2("win2", LIST2, LIST2 + 512), [[0, 512]], 256, 0)
+    for n, sh, m in (("b2", 2, 1), ("qi", 0, 15), ("gi", 4, 7)):
+        ts(one(n), one("pc"), sh, A.arith_shift_right, m, A.bitwise_and)
+    for b in range(2):
+        tt(v2("sb%d" % b, 0, 32), v2("sb%d" % b, 0, 32), v2("hm", 0, 32), A.mult)
+    ts(one("q4"), one("qi"), 4.0, A.mult)
+    ts(one("t0b"), one("b2"), TINY, A.mult)
+    cp(one("gf"), one("gi"))
+    ts(v2("am", 128, 129), one("b4"), -1.0, A.mult, 1.0, A.add)
+    fill(v2("a2", 0, 64, 4), LOW)
+    ts(v2("offct", 0, 32), v2("ctb", 0, 32), one("q4"), A.add)
     act(v2("p2f", 0, 8), v2("p2b", 0, 8), ACT.Copy)
     for b in range(2):
         for t in range(4):
-            act(plane_cols("w2t", b, t), v2("sg%d" % b, 0, 16), ACT.Copy, scale=v2("p2f", 4 * b + t, 4 * b + t + 1))
-    for n, sh, m in (("qi", 0, 15), ("gi", 4, 7), ("oi", 0, 1)):
-        ts(one(n), one("pc"), sh, A.arith_shift_right, m, A.bitwise_and)
-    ts(one("q4"), one("qi"), 4.0, A.mult)
-    ts(one("evf"), one("oi"), -1.0, A.mult, 1.0, A.add)
-    ts(one("t15"), one("oi"), -15.0, A.mult, 16.0, A.add)
-    cp(one("oddf"), one("oi"))
-    ts(v2("ctf", 0, 32), v2("ctb", 0, 32), one("q4"), A.add)
-    tt(one("hc"), one("t15"), one("b4"), A.mult)
-    cp(v2("offct", 0, 32), v2("ctf", 0, 32))
-    act(v2("va", 0, 256), v2("plc", 0, 256), ACT.Identity, bias=one("hc"), scale=one("evf"))
-    act(v2("vp", 0, 256), v2("pib", 0, 256), ACT.Copy, scale=one("oddf"))
+            act(plane_cols(2, b, t), v2("sb%d" % b, 0, 32), ACT.Copy, scale=v2("p2f", 4 * b + t, 4 * b + t + 1))
+    act(v2("X", 0, 64), v2("zt", 0, 64), ACT.Identity, bias=8.0)
+    act(v2("f8", 0, 32), v2("c8", 0, 32), ACT.Sign)
+    act(v2("f16", 0, 64), v2("q16", 0, 64), ACT.Sign)
+    act(v2("tabrow", 512, 520), v2("zt", 0, 8), ACT.Copy)
+    act(v2("idp", 0, 32), v2("zt", 0, 32), ACT.Copy)
+    act(v2("val2", 0, 256), v2("plc", 0, 256), ACT.Identity, bias=one("h16"))
     quant("wvq", 0, 512, "wvb", 0)
-    quant("w2", 0, 136, "w2t", 0)
-    quant("w2", 136, 272, "w2t", 544)
-    ts(one("out2"), one("evf"), LOW, A.mult)
-    ts(one("kk"), one("bb"), 512.0, A.mult, float(DUMP), A.add)
-    cp(one("qf"), one("qi"))
-    cp(one("gf"), one("gi"))
-    ts(one("thr2"), one("out2"), one("thrm"), A.add, TINY, A.add)
-    tt(one("init2"), one("kk"), one("j0"), A.mult)
-    fill(v2("X", 0, 32), 0.0)
-    fill(v2("X", 9, 32, 2), 8.0)
-    fill(v2("tabrow", 512, 520), 0.0)
-    fill(v2("idp", 0, 32), 0.0)
+    quant("w2", 0, 144, "w2t", 0)
+    quant("w2", 144, 288, "w2t", 576)
     quant("hq", 512, 640, "zt", 0)
+    ts(v2("dmp", 0, 16), v2("c64", 0, 16), one("q4"), A.add, 0.0625, A.mult)
     ts(v2("dm1", 0, 32), v2("c8", 0, 32), one("gf"), A.is_equal)
-    ts(v2("dm2", 0, 64), v2("q16", 0, 64), one("qf"), A.is_equal)
-    ts(v2("f8", 0, 32), v2("c8", 0, 32), 0.0, A.not_equal)
-    ts(v2("f16", 0, 64), v2("q16", 0, 64), 0.0, A.not_equal)
-    tt(v2("val2", 0, 256), v2("va", 0, 256), v2("vp", 0, 256), A.add)
+    ts(v2("dm2", 0, 64), v2("q16", 0, 64), one("q4"), A.is_equal)
 
     for s in range(N):
         if s != rank:
@@ -399,9 +398,11 @@ def rank_program(g, core, T, topo):
             ts(v2("fF", 0, 32), v2("nl", 0, 32), 255.5, A.is_lt)
             cp(v2("nf", 0, 32), v2("nl", 0, 32))
             for m in range(4):
-                total_of(v2("X", 1 + 2 * m, 2 + 2 * m), v2("fF", 8 * m, 8 * m + 8))
+                x = 32 * (m % 2) + 12 + 16 * (m // 2)
+                total_of(v2("X", x, x + 1), v2("fF", 8 * m, 8 * m + 8))
             tt(v2("nt", 0, 32), v2("nf", 0, 32), v2("nadd", 0, 32), A.add)
-    dma("s", "ltb", (T.tabrow[0:1, 0:512], v2("tabrow", 0, 512)[1], []), (T.nt[0:16, 0:32], v2("nt", 0, 32)[1], []))
+            turn32(v2("ntt", 0, 32), v2("nt", 0, 32))
+    dma("s", "ltb", (T.tabrow[0:1, 0:512], v2("tabrow", 0, 512)[1], []), (T.ntt[0:32, 0:16], v2("ntt", 0, 32)[1], []))
     do("g", "partition_broadcast", v2("tab", 0, 520), (T.tabrow[0:1, 0:520], v2("tabrow", 0, 520)[1], []), 128)
     quant("vq", 0, 512, "vt", 0)
     for h, who in enumerate(("aaaa", "aaav")):
@@ -415,34 +416,57 @@ def rank_program(g, core, T, topo):
             mm(b0 + i, n, "vq", 128 * i, "aq", lo)
         if lo == 384:
             for b in (1, 0):
-                for m in range(3):
-                    mm(b, 128, "w2", 136 * b + 6 - 2 * m, "hq", 128 * m, m == 0, False)
+                mm(b, 128, "w2", 144 * b + 16, "hq", 0, True, False)
+                mm(b, 128, "w2", 144 * b, "hq", 256, False, True)
+            for b in (1, 0):
+                mm(2 + b, 128, "w2", 144 * b + 16, "hq", 128, True, False)
         for i in range(4):
             empty(who[i], "ht", 4 * lo, i, b0 + i, n, "scale")
         if lo == 0:
-            turn32(v2("xt", 0, 32), v2("X", 0, 32))
-            total_of(one("cnt2"), v2("xt", 0, 32))
+            turn32(v2("xt", 0, 64), v2("X", 0, 64))
+            for h in range(2):
+                total_of(one("cnt%d" % h), v2("xt", 32 * h, 32 * h + 32))
         quant("hq", lo, lo + n, "ht", 4 * lo)
+        if lo == 0:
+            for h in range(2):
+                ts(half("tb2", h), v2("io2", 0, 128), one("cnt%d" % h), A.is_lt, one("t0a"), A.mult)
     for b in (1, 0):
-        mm(b, 128, "w2", 136 * b, "hq", 384, False, True)
+        mm(2 + b, 128, "w2", 144 * b, "hq", 384, False, True)
 
-    ts(f128("te"), f128("io2"), one("cnt2"), A.is_ge, HIGH, A.mult)
-    ts(f128("bm"), f128("te"), one("bias"), A.add)
-    places(2, 16, f128("bm"), one("thr2"))
-    tt(v3("dst2", 0, 4, 0, 4), v3("F2", 0, 4, 0, 4), v3("dumpc", 0, 4, 0, 4), A.max)
-    cp(v2("do2", 0, 16), v3("dst2", 0, 4, 0, 4))
-    cp(by(v2("win2", 0, 2448), v2("do2", 0, 16)), v2("val2", 0, 256))
-    for half in range(2):
-        a, b = 16 * half, 16 * half + 16
-        lists(half, "win2", DUMP + 1, 512, "wd2", "t22")
-        tt(v3("l2", a, b, 0, 2), v3("t22", a, b, 0, 2), v3("t22", a, b, 16, 18), A.add)
-        cp(v2("off2", a, b), v3i("l2", a, b, 0))
-        if half == 0:
+    def sign(h):
+        act(half("J2", h), half("ind2", h), ACT.Identity, scale=2 * FAR, bias=-FAR)
+
+    gate(2, 0)
+    member(2, 0)
+    scan(v2("C2", 0, 128), v2("am", 0, 128), v2("ind2", 0, 128), 0.0, A.mult, A.add)
+    sign(0)
+    gate(2, 1)
+    member(2, 1)
+    sign(1)
+    turn32(v2("tC2", 0, 128), v2("C2", 0, 128))
+    scan(v2("C2", 128, 416), v2("am", 0, 288), v2("ind2", 128, 416), v2("C2", 127, 128), A.mult, A.add)
+    turn32(half("tJ2", 0), half("J2", 0))
+    turn32(v2("tC2", 128, 416), v2("C2", 128, 416))
+    turn32(half("tJ2", 1), half("J2", 1))
+    for h in range(2):
+        tt(v2("D2", 32 * h, 32 * h + 32), v2("tC2", 128 * h, 128 * h + 128, 4), v2("tC2", 272, 400, 4), A.add)
+    tt(v2("M2", 0, 64), v2("D2", 0, 64), v2("tJ2", 0, 256, 4), A.min)
+    scan(v2("R2", 0, 64), v2("a2", 0, 64), v2("M2", 0, 64), 0.0, A.add, A.max)
+    tt(v2("dst2", 0, 16), v2("R2", 3, 64, 4), v2("dmp", 0, 16), A.max)
+    ts(v2("do2", 0, 16), v2("dst2", 0, 16), 4.0, A.mult, 256.0, A.add)
+    cp(by(v2("win2", 0, 2320), v2("do2", 0, 16)), v2("val2", 0, 256))
+    spread("win2", LIST2, "wd2")
+    for hf in range(2):
+        a, b = 16 * hf, 16 * hf + 16
+        turn32(v3("t22", a, b, 0, 32), v3("wd2", a, b, 0, 32))
+        tt(v2("l2", a, b), v3i("t22", a, b, 0), v3i("t22", a, b, 16), A.add)
+        cp(v2("off2", a, b), v2("l2", a, b))
+        if hf == 0:
             pick("slotb", 0, 256, "hq", 640, "off2", 0)
         else:
+            tt(v2("pd", 0, 32), v2("l2", 0, 32), v2("dm1", 0, 32), A.mult)
             pick("slotb", 256, 384, "hq", 640, "off2", 2)
-        send_cols(far_ks if half == 0 else near_ks, "c2_%d" % rank, "s2_%d" % rank, "slotb", "landb")
-    tt(v2("pd", 0, 32), v3i("l2", 0, 32, 1), v2("dm1", 0, 32), A.mult)
+        send_cols(far_ks if hf == 0 else near_ks, "c2_%d" % rank, "s2_%d" % rank, "slotb", "landb")
     scan(v2("pds", 0, 32), v2("f8", 0, 32), v2("pd", 0, 32), 0.0, A.mult, A.add)
     cp(v2("offD", 0, 4), v2("pds", 7, 32, 8))
     cp(v2("ga", 0, 64), by(v2("tab", 0, 520), v2("offD", 0, 4)))
@@ -460,9 +484,15 @@ def rank_program(g, core, T, topo):
             arrive("s2_%d" % s, share[s], plane("landb", 128 * s, 128 * s + 128))
             arrive("n2", every, v2("idl", 8 * s, 8 * s + 1))
     turn = [rank] + near + off
-    for s in turn:
-        dma("s", "oc%d" % s, ext(T.oc[:, 512 * s:512 * s + 512]), codes("landb", 128 * s, 128 * s + 128, dt.uint8))
+
+    def store_codes(q, s):
+        dma(q, "oc%d" % s, ext(T.oc[:, 512 * s:512 * s + 512]), codes("landb", 128 * s, 128 * s + 128, dt.uint8))
+
+    for s in [rank] + off:
+        store_codes("s", s)
     for i, s in enumerate(turn):
+        if s in near:
+            store_codes("a", s)
         bank = (6, 7, 2, 3)[i]
         mm(bank, 128, "wq", 0, "landb", 128 * s)
         o, z = v2("yb", 128 * s, 128 * s + 128), v2("ps%d" % bank, 0, 128)

@@ -19,7 +19,7 @@ for _n, _w, _t in (
         ("l1", 32, F), ("l2", 32, F),
         ("g2", 256, B), ("ind2", 416, B), ("C2", 416, B), ("J2", 256, B), ("tJ2", 256, B), ("tC2", 416, B), ("D2", 64, F),
         ("M2", 64, F), ("R2", 64, F), ("dst2", 16, F),
-        ("pd", 32, F), ("pds", 32, F), ("ga", 64, F), ("gm", 64, F), ("gms", 64, F), ("idp", 32, F),
+        ("pd", 32, F), ("pds", 32, F), ("gm", 64, F), ("gms", 64, F), ("idp", 32, F),
         ("idt", 32, F), ("yb", 512, F),
         ("do1", 8, U), ("do2", 16, U), ("off1", 32, U), ("off2", 32, U), ("offct", 32, U), ("offD", 4, U), ("nl", 32, U),
         ("idu", 4, U), ("idl", 32, U)):
@@ -288,9 +288,14 @@ def rank_program(g, core, T, topo):
         o = half("g%d" % k, h)
         if k == 1:
             ts(o, prod(h, 1), one("t1a"), A.is_ge, LOW, A.mult)
-            ts(o, o, one("t0a"), A.add)
         else:
             tt(o, prod(h, 1), half("tb2", h), A.is_ge)
+
+    def bound(k, h):
+        o = half("g%d" % k, h)
+        if k == 1:
+            ts(o, o, one("t0a"), A.add)
+        else:
             ts(o, o, LOW, A.mult, one("t0b"), A.add)
 
     def member(k, h):
@@ -300,8 +305,10 @@ def rank_program(g, core, T, topo):
         scan(half("C1", h), half("ind1", h), v2("zt", 0, 128), v2("C1", 127, 128) if h else 0.0, A.add, A.add)
 
     gate(1, 0)
-    member(1, 0)
+    bound(1, 0)
     gate(1, 1)
+    member(1, 0)
+    bound(1, 1)
     count1(0)
     member(1, 1)
     turn32(half("tI1", 0), half("ind1", 0))
@@ -411,7 +418,7 @@ def rank_program(g, core, T, topo):
             mm(bank, 256, "ct", 128 * t, "landa", 256 * h)
             empty(who[t], "at", 1024 * h, t, bank, 256, "relu")
         quant("aq", 256 * h, 256 * h + 256, "at", 1024 * h)
-    for lo, n, b0, who in ((0, 256, 4, "aava"), (256, 128, 0, "aava"), (384, 128, 4, "avav")):
+    for lo, n, b0, who in ((0, 256, 4, "aava"), (256, 128, 0, "aaaa"), (384, 128, 4, "avav")):
         for i in range(4):
             mm(b0 + i, n, "vq", 128 * i, "aq", lo)
         if lo == 384:
@@ -437,17 +444,19 @@ def rank_program(g, core, T, topo):
         act(half("J2", h), half("ind2", h), ACT.Identity, scale=2 * FAR, bias=-FAR)
 
     gate(2, 0)
-    member(2, 0)
-    scan(v2("C2", 0, 128), v2("am", 0, 128), v2("ind2", 0, 128), 0.0, A.mult, A.add)
-    sign(0)
+    bound(2, 0)
     gate(2, 1)
+    member(2, 0)
+    sign(0)
+    bound(2, 1)
+    scan(v2("C2", 0, 128), v2("am", 0, 128), v2("ind2", 0, 128), 0.0, A.mult, A.add)
     member(2, 1)
     sign(1)
     turn32(v2("tC2", 0, 128), v2("C2", 0, 128))
     scan(v2("C2", 128, 416), v2("am", 0, 288), v2("ind2", 128, 416), v2("C2", 127, 128), A.mult, A.add)
     turn32(half("tJ2", 0), half("J2", 0))
-    turn32(v2("tC2", 128, 416), v2("C2", 128, 416))
     turn32(half("tJ2", 1), half("J2", 1))
+    turn32(v2("tC2", 128, 416), v2("C2", 128, 416))
     for h in range(2):
         tt(v2("D2", 32 * h, 32 * h + 32), v2("tC2", 128 * h, 128 * h + 128, 4), v2("tC2", 272, 400, 4), A.add)
     tt(v2("M2", 0, 64), v2("D2", 0, 64), v2("tJ2", 0, 256, 4), A.min)
@@ -469,8 +478,7 @@ def rank_program(g, core, T, topo):
         send_cols(far_ks if hf == 0 else near_ks, "c2_%d" % rank, "s2_%d" % rank, "slotb", "landb")
     scan(v2("pds", 0, 32), v2("f8", 0, 32), v2("pd", 0, 32), 0.0, A.mult, A.add)
     cp(v2("offD", 0, 4), v2("pds", 7, 32, 8))
-    cp(v2("ga", 0, 64), by(v2("tab", 0, 520), v2("offD", 0, 4)))
-    tt(v2("gm", 0, 64), v2("ga", 0, 64), v2("dm2", 0, 64), A.mult)
+    tt(v2("gm", 0, 64), by(v2("tab", 0, 520), v2("offD", 0, 4)), v2("dm2", 0, 64), A.mult)
     scan(v2("gms", 0, 64), v2("f16", 0, 64), v2("gm", 0, 64), 0.0, A.mult, A.add)
     cp(v2("idu", 0, 4), v2("gms", 15, 64, 16))
     send(all_ks, "n2", [(v2("idu", k, k + 1), v2("idl", 8 * rank, 8 * rank + 1)) for k in all_ks])

from concourse.bass import DstId, RemoteDMATransfer
from concourse.mybir import dt, AluOpType, AxisListType, ActivationFunctionType

F, B, I, U = "float32", "bfloat16", "int32", "uint16"
Q, S8 = "float8_e4m3fn_x4", "uint8"
COL = {n: ("ki", k) for k, n in enumerate(("pc", "b2", "b3", "b4", "qi", "gi"))}
COL.update({n: ("kf", k) for k, n in enumerate(("t0a", "t1a", "t0b", "h16", "q4", "gf", "cnt0", "cnt1"))})
SCRATCH = {}
for _n, _w, _t in (
        ("plb", 8, B), ("p2b", 8, B), ("p1f", 8, F), ("p2f", 8, F), ("xb", 1024, B), ("wvb", 2048, B), ("wb", 512, B),
        ("w1t", 1024, B), ("zt", 576, B), ("w2t", 1152, B), ("at", 2048, B), ("vt", 2048, B), ("ht", 2048, B),
        ("sa0", 16, B), ("sa1", 16, B), ("sb0", 32, B), ("sb1", 32, B), ("hm", 32, B),
        ("val1", 128, B), ("val2", 256, B), ("win1", 1040, B), ("win2", 2320, B), ("ki", 16, I), ("kf", 24, F),
        ("vb1", 128, F), ("ctb", 32, F), ("plc", 256, F), ("c8", 32, F), ("dm1", 32, F), ("f8", 32, F), ("q16", 64, F),
        ("dm2", 64, F), ("f16", 64, F), ("io2", 128, B), ("nadd", 32, F), ("X", 64, F), ("xt", 64, F), ("fF", 32, F),
        ("nf", 32, F), ("nt", 32, F), ("ntt", 32, F), ("tb2", 256, B), ("am", 288, B), ("a1", 32, F), ("a2", 64, F),
        ("c64", 16, F), ("dmp", 16, F), ("tabrow", 520, F), ("tab", 520, F),
        ("g1", 256, B), ("ind1", 256, B), ("C1", 256, B), ("tI1", 256, B), ("tC1", 256, B), ("M1", 32, F), ("R1", 32, F),
        ("l1", 32, F), ("l2", 32, F),
        ("g2", 256, B), ("ind2", 416, B), ("C2", 416, B), ("J2", 256, B), ("tJ2", 256, B), ("tC2", 416, B), ("D2", 64, F),
        ("M2", 64, F), ("R2", 64, F), ("dst2", 16, F),
        ("pd", 32, F), ("pds", 32, F), ("gm", 64, F), ("gms", 64, F), ("idp", 32, F),
        ("idt", 32, F), ("yb", 512, F),
        ("do1", 8, U), ("do2", 16, U), ("off1", 32, U), ("off2", 32, U), ("offct", 32, U), ("offD", 4, U), ("nl", 32, U),
        ("idu", 4, U), ("idl", 32, U)):
    SCRATCH[_n] = ("sbuf", [128, _w], _t)
for _n in ("wd1", "t21", "wd2", "t22"):
    SCRATCH[_n] = ("sbuf", [128, 32, 32], B)
for _n, _w in (("w1", 256), ("xq", 384), ("slota", 384), ("landa", 512), ("ct", 512), ("wvq", 512), ("aq", 512), ("vq", 512),
               ("w2", 288), ("hq", 640), ("slotb", 384), ("landb", 512), ("wq", 128)):
    SCRATCH[_n + "c"] = ("sbuf", [128, _w], Q)
    SCRATCH[_n + "s"] = ("sbuf", [128, _w], S8)
for _k in range(8):
    SCRATCH["ps%d" % _k] = ("psum", [128, 512], F)

SEMAPHORES = (["sv", "sa", "sp", "sg", "sent", "c1", "n1", "n2", "lpl", "lx0", "lx1", "lp2", "lwv", "lw", "ltb"]
              + ["%s_%d" % (n, k) for n in ("c2", "s2") for k in range(4)]
              + ["%s%d" % (n, k) for n in ("oc", "os", "yy", "ii") for k in range(4)])

TINY = 2.0 ** -120
LOW, FAR = -2.0 ** 99, 2.0 ** 20
LIST1, LIST2 = 4, 260


def rank_program(g, core, T, topo):
    rank = T.rank_of(core)
    if rank is None:
        return
    N = len(T.cores)
    A, ACT = AluOpType, ActivationFunctionType
    eng = {"v": g.vector, "a": g.scalar, "p": g.tensor, "g": g, "s": g.sync}
    csem = {"v": "sv", "a": "sa", "p": "sp", "g": "sg"}
    total, waited, know, acc = {}, {}, {q: {} for q in eng}, {}

    def clash(x, y):
        if x[1] >= y[2] or y[1] >= x[2]:
            return False
        if x[3] == y[3] and x[3] > 1:
            a, b = x[1] % x[3], y[1] % y[3]
            return a < b + y[4] and b < a + x[4]
        return True

    def order(q, tok):
        sem, n, clock = tok
        k = know[q]
        if k.get(sem, 0) < n:
            eng[q].wait_ge(T.sem[sem], n)
            waited[sem] = max(waited.get(sem, 0), n)
            k[sem] = n
        for s, m in clock.items():
            if k.get(s, 0) < m:
                k[s] = m

    def touch(q, reads, writes):
        todo = []
        for kind, specs in ((0, reads), (1, writes)):
            for sp in specs:
                for old, okind, tok, oq in acc.get(sp[0], ()):
                    if sp[0][:2] == "ps":
                        if oq != q:
                            todo.append(tok)
                    elif (kind or okind) and clash(sp, old):
                        todo.append(tok)
        todo.sort(key=lambda t: (t[0], -t[1]))
        for t in todo:
            order(q, t)

    def note(q, tok, reads, writes):
        for kind, specs in ((0, reads), (1, writes)):
            for sp in specs:
                acc.setdefault(sp[0], []).append((sp, kind, tok, q))

    def v2(name, a, b, step=1):
        return (T[name][:, a:b:step] if step > 1 else T[name][:, a:b], [(name, a, b, step, 1)], [])

    def half(name, h):
        return v2(name, 128 * h, 128 * h + 128)

    def one(n):
        return v2(COL[n][0], COL[n][1], COL[n][1] + 1)

    def v3(name, a, b, c, d):
        w = SCRATCH[name][1][2]
        return (T[name][:, a:b, c:d], [(name, a * w + c, (b - 1) * w + d, w, d - c)], [])

    def v3i(name, a, b, c):
        w = SCRATCH[name][1][2]
        return (T[name][:, a:b, c], [(name, a * w + c, (b - 1) * w + c + 1, w, 1)], [])

    def codes(name, a, b, bits=None):
        ap = T[name + "c"][:, a:b]
        return (ap.bitcast(bits) if bits else ap, [(name + "c", a, b, 1, 1)], [])

    def plane(name, a, b):
        return v2(name + "s", a, b)

    def by(win, off):
        return (win[0].indirect(off[0]), win[1], off[1])

    calls = {"tensor_copy": g.vector.tensor_copy, "tensor_tensor": g.vector.tensor_tensor, "memset": g.vector.memset,
             "tensor_reduce": g.vector.tensor_reduce, "tensor_scalar": g.vector.tensor_scalar,
             "tensor_tensor_scan": g.vector.tensor_tensor_scan, "transpose": g.vector.transpose,
             "quantize_mx": g.vector.quantize_mx, "activation": g.scalar.activation, "matmul_mx": g.tensor.matmul_mx,
             "iota": g.iota, "partition_broadcast": g.partition_broadcast}

    def do(q, call, *args, outs=1, **kw):
        reads, writes, plain = [], [], []
        for i, x in enumerate(args):
            if isinstance(x, tuple):
                (writes if i < outs else reads).extend(x[1])
                reads.extend(x[2])
                plain.append(x[0])
            else:
                plain.append(x)
        for k in kw:
            if isinstance(kw[k], tuple):
                reads.extend(kw[k][1])
                kw[k] = kw[k][0]
        touch(q, reads, writes)
        s = csem[q]
        calls[call](*plain, **kw).then_inc(T.sem[s], 1)
        total[s] = total.get(s, 0) + 1
        note(q, (s, total[s], dict(know[q])), reads, writes)

    def dma(q, sem, out, in_):
        touch(q, in_[1], out[1])
        eng[q].dma_start(out[0], in_[0]).then_inc(T.sem[sem], 16)
        total[sem] = 16
        note(q, (sem, 16, dict(know[q])), in_[1], out[1])

    def ext(ap):
        return (ap, [], [])

    def arrive(sem, n, *specs):
        total[sem] = n
        for sp in specs:
            note("far", (sem, n, {}), [], sp[1])

    def tt(out, a, b, op):
        do("v", "tensor_tensor", out, a, b, op)

    def ts(out, a, s1, op0, s2=None, op1=None):
        if op1 is None:
            do("v", "tensor_scalar", out, a, s1, None, op0)
        else:
            do("v", "tensor_scalar", out, a, s1, s2, op0, op1)

    def cp(out, a):
        do("v", "tensor_copy", out, a)

    def act(out, a, f, **kw):
        do("a", "activation", out, a, f, **kw)

    def fill(out, c):
        do("v", "memset", out, c)

    def scan(out, a, b, init, op0, op1):
        do("v", "tensor_tensor_scan", out, a, b, init, op0, op1)

    def turn32(out, a):
        do("v", "transpose", out, a)

    def total_of(out, a):
        do("v", "tensor_reduce", out, a, AxisListType.X, A.add)

    def quant(name, a, b, tile, lo):
        do("v", "quantize_mx", codes(name, a, b), plane(name, a, b), v2(tile, lo, lo + 4 * (b - a)), outs=2)

    def mm(bank, n, l, la, r, ra, start=True, stop=True):
        do("p", "matmul_mx", v2("ps%d" % bank, 0, n), codes(l, la, la + 128), plane(l, la, la + 128),
           codes(r, ra, ra + n), plane(r, ra, ra + n), start, stop)

    def iota(out, pattern, base, cm, flag=True):
        if flag:
            do("g", "iota", out, pattern, base, cm, allow_small_or_imprecise_dtypes=True)
        else:
            do("g", "iota", out, pattern, base, cm)

    off = [r for r in range(N) if r != rank and topo.chip(T.cores[r]) != topo.chip(core)]
    near = [r for r in range(N) if r != rank and topo.chip(T.cores[r]) == topo.chip(core)]
    perm = off + near + [rank]
    share = {r: 8 if r in near else 4 for r in off + near}
    every = sum(share.values())
    used, mask = [], {}
    for r in off + near:
        es = [e for e in topo.engines(core, T.cores[r]) if e not in used][:share[r]]
        used += es
        mask[r] = sum(1 << e for e in es)
    sent = [0]

    def send(ks, sem, pairs):
        trs = []
        for k, (src, dst) in zip(ks, pairs):
            touch("g", src[1], [])
            rid, pid = topo.addr(T.cores[perm[k]])[:2]
            trs.append(RemoteDMATransfer(dst_ids=[DstId(rid=rid, pnc=pid)], dma_engine_mask=mask[perm[k]],
                                         remote_sem=T.sem[sem], src=src[0], dst=dst[0]))
            sent[0] += share[perm[k]]
        g.remote_dma_fused(trs, local_sem=T.sem.sent)

    def send_cols(ks, sem, sem2, slot, land):
        u8 = dt.uint8
        send(ks, sem, [(codes(slot, 128 * k, 128 * k + 128, u8), codes(land, 128 * rank, 128 * rank + 128, u8)) for k in ks])
        send(ks, sem2, [(plane(slot, 128 * k, 128 * k + 128), plane(land, 128 * rank, 128 * rank + 128)) for k in ks])

    far_ks, near_ks = list(range(len(off))), list(range(len(off), N - 1))
    all_ks = far_ks + near_ks

    dma("s", "lpl", v2("plb", 0, 8), ext(T.pl[:, 0:8]))
    dma("a", "lx0", v2("xb", 0, 512), ext(T.x[:, 0:512]))
    dma("s", "lx1", v2("xb", 512, 1024), ext(T.x[:, 512:1024]))
    touch("s", v2("xb", 0, 1024)[1], [])
    dma("s", "lp2", v2("p2b", 0, 8), ext(T.p2[:, 0:8]))
    dma("s", "lwv", v2("wvb", 0, 2048), ext(T.wv[:]))
    dma("s", "lw", v2("wb", 0, 512), ext(T.w[:]))

    iota(one("pc"), [[0, 1]], 0, 1, False)
    iota(v2("sa1", 0, 16), [[0, 4], [-2, 2], [0, 2]], 1, 0)
    iota(v2("sa0", 0, 16), [[0, 8], [-2, 2]], 1, 0)
    iota(v2("vb1", 0, 128), [[32, 8], [1, 16]], -128, 0)
    iota(v2("ctb", 0, 32), [[1, 4], [64, 8]], 0, 0)
    iota(v2("c8", 0, 32), [[0, 4], [1, 8]], 0, 0)
    iota(v2("q16", 0, 64), [[0, 4], [4, 16]], 0, 0)
    iota(v2("nadd", 0, 32), [[256, 4], [0, 8]], 1, 0)
    iota(v2("sb0", 0, 32), [[0, 16], [-2, 2]], 1, 0)
    iota(v2("sb1", 0, 32), [[0, 8], [-2, 2], [0, 2]], 1, 0)
    iota(v2("hm", 0, 32), [[0, 4], [-1, 2], [0, 4]], 1, 0)
    iota(v2("c64", 0, 16), [[64, 16]], -1024, 0)

    fill(v2("zt", 0, 576), 0.0)
    fill(v2("w1t", 512, 1024), 0.0)
    for n, sh in (("b4", 4), ("b3", 3)):
        ts(one(n), one("pc"), sh, A.arith_shift_right, 1, A.bitwise_and)
    ts(one("t1a"), one("b4"), TINY, A.mult)
    ts(one("t0a"), one("b3"), TINY, A.mult)
    ts(one("h16"), one("b4"), 16.0, A.mult)
    quant("xq", 256, 384, "zt", 0)
    fill(v2("a1", 0, 32), 0.25)
    fill(v2("a1", 0, 32, 4), LOW)

    def plane_cols(k, b, t):
        return v2("w1t", 512 * b + t, 512 * b + 512, 32) if k == 1 else v2("w2t", 576 * b + 64 + t, 576 * b + 564, 16)

    act(v2("w1t", 0, 512), v2("zt", 0, 512), ACT.Copy)
    act(v2("p1f", 0, 8), v2("plb", 0, 8), ACT.Copy)
    for t in range(4):
        act(plane_cols(1, 0, t), v2("sa0", 0, 16), ACT.Copy, scale=v2("p1f", t, t + 1))
    act(v2("val1", 0, 128), v2("vb1", 0, 128), ACT.Identity, bias=one("h16"))
    act(v2("win1", LIST1, LIST1 + 516), v2("zt", 0, 516), ACT.Identity, bias=128.0)
    for b in range(2):
        act(v2("w2t", 576 * b, 576 * b + 576), v2("zt", 0, 576), ACT.Copy)
    act(v2("ind2", 256, 416), v2("zt", 0, 160), ACT.Copy)
    act(v2("am", 0, 288), v2("zt", 0, 288), ACT.Identity, bias=1.0)
    act(v2("a2", 0, 64), v2("zt", 0, 64), ACT.Identity, bias=0.25)
    for t in range(4):
        ts(plane_cols(1, 1, t), v2("sa1", 0, 16), v2("plb", 4 + t, 5 + t), A.mult)

    quant("w1", 128, 256, "w1t", 512)
    quant("xq", 0, 128, "xb", 0)
    quant("w1", 0, 128, "w1t", 0)
    quant("xq", 128, 256, "xb", 512)
    for h in range(2):
        for b in (1, 0):
            mm(2 * h + b, 128, "w1", 128 * b, "xq", 128 * h)
    prod = lambda h, b: v2("ps%d" % (2 * h + b), 0, 128)

    def gate(k, h):
        o = half("g%d" % k, h)
        if k == 1:
            ts(o, prod(h, 1), one("t1a"), A.is_ge, LOW, A.mult)
        else:
            tt(o, prod(h, 1), half("tb2", h), A.is_ge)

    def bound(k, h):
        o = half("g%d" % k, h)
        if k == 1:
            ts(o, o, one("t0a"), A.add)
        else:
            ts(o, o, LOW, A.mult, one("t0b"), A.add)

    def member(k, h):
        tt(half("ind%d" % k, h), prod(h, 0), half("g%d" % k, h), A.is_lt)

    def count1(h):
        scan(half("C1", h), half("ind1", h), v2("zt", 0, 128), v2("C1", 127, 128) if h else 0.0, A.add, A.add)

    gate(1, 0)
    bound(1, 0)
    gate(1, 1)
    member(1, 0)
    bound(1, 1)
    count1(0)
    member(1, 1)
    turn32(half("tI1", 0), half("ind1", 0))
    count1(1)
    turn32(half("tC1", 0), half("C1", 0))
    turn32(half("tI1", 1), half("ind1", 1))
    turn32(half("tC1", 1), half("C1", 1))
    tt(v2("M1", 0, 32), v2("tI1", 0, 256, 8), v2("tC1", 0, 256, 8), A.mult)
    scan(v2("R1", 0, 32), v2("a1", 0, 32), v2("M1", 0, 32), 0.0, A.add, A.max)
    ts(v2("do1", 0, 8), v2("R1", 3, 32, 4), 4.0, A.mult)
    cp(by(v2("win1", 0, 1040), v2("do1", 0, 8)), v2("val1", 0, 128))

    def spread(win, lo, wd):
        for k in range(4):
            for h in range(2):
                o, z = v3(wd, 8 * k, 8 * k + 8, 16 * h, 16 * h + 16), v2(win, lo + perm[k], lo + perm[k] + 509, 4)
                if k > 1 or k + h == 0:
                    act(o, z, ACT.Copy)
                else:
                    cp(o, z)

    def pick(dst, a, b, src, w, offs, k):
        o = v2(offs, 8 * k, 8 * k + (b - a) // 16)
        cp(codes(dst, a, b, dt.uint32), by(codes(src, 0, w, dt.uint32), o))
        act(plane(dst, a, b), by(plane(src, 0, w), o), ACT.Copy)

    spread("win1", LIST1, "wd1")
    for hf in range(2):
        a, b = 16 * hf, 16 * hf + 16
        turn32(v3("t21", a, b, 0, 32), v3("wd1", a, b, 0, 32))
        tt(v2("l1", a, b), v3i("t21", a, b, 0), v3i("t21", a, b, 16), A.add)
        cp(v2("off1", a, b), v2("l1", a, b))
        if hf == 0:
            pick("slota", 0, 256, "xq", 384, "off1", 0)
        else:
            pick("slota", 256, 384, "xq", 384, "off1", 2)
        send_cols(far_ks if hf == 0 else near_ks, "c1", "c1", "slota", "landa")
    send(all_ks, "n1", [(v2("off1", 8 * k, 8 * k + 8), v2("nl", 8 * rank, 8 * rank + 8)) for k in all_ks])
    pick("landa", 128 * rank, 128 * rank + 128, "xq", 384, "off1", 3)
    cp(v2("nl", 8 * rank, 8 * rank + 8), v2("off1", 24, 32))

    for h in range(2):
        iota(half("plc", h), [[32, 4], [256, 2], [1, 16]], 128 * h - 256, 0)
    iota(v2("io2", 0, 128), [[2, 128]], 0, 0)
    iota(v2("win2", LIST2, LIST2 + 512), [[0, 512]], 256, 0)
    for n, sh, m in (("b2", 2, 1), ("qi", 0, 15), ("gi", 4, 7)):
        ts(one(n), one("pc"), sh, A.arith_shift_right, m, A.bitwise_and)
    for b in range(2):
        tt(v2("sb%d" % b, 0, 32), v2("sb%d" % b, 0, 32), v2("hm", 0, 32), A.mult)
    ts(one("q4"), one("qi"), 4.0, A.mult)
    ts(one("t0b"), one("b2"), TINY, A.mult)
    cp(one("gf"), one("gi"))
    ts(v2("am", 128, 129), one("b4"), -1.0, A.mult, 1.0, A.add)
    fill(v2("a2", 0, 64, 4), LOW)
    ts(v2("offct", 0, 32), v2("ctb", 0, 32), one("q4"), A.add)
    act(v2("p2f", 0, 8), v2("p2b", 0, 8), ACT.Copy)
    for b in range(2):
        for t in range(4):
            act(plane_cols(2, b, t), v2("sb%d" % b, 0, 32), ACT.Copy, scale=v2("p2f", 4 * b + t, 4 * b + t + 1))
    act(v2("X", 0, 64), v2("zt", 0, 64), ACT.Identity, bias=8.0)
    act(v2("f8", 0, 32), v2("c8", 0, 32), ACT.Sign)
    act(v2("f16", 0, 64), v2("q16", 0, 64), ACT.Sign)
    act(v2("tabrow", 512, 520), v2("zt", 0, 8), ACT.Copy)
    act(v2("idp", 0, 32), v2("zt", 0, 32), ACT.Copy)
    act(v2("val2", 0, 256), v2("plc", 0, 256), ACT.Identity, bias=one("h16"))
    quant("wvq", 0, 512, "wvb", 0)
    quant("w2", 0, 144, "w2t", 0)
    quant("w2", 144, 288, "w2t", 576)
    quant("hq", 512, 640, "zt", 0)
    ts(v2("dmp", 0, 16), v2("c64", 0, 16), one("q4"), A.add, 0.0625, A.mult)
    ts(v2("dm1", 0, 32), v2("c8", 0, 32), one("gf"), A.is_equal)
    ts(v2("dm2", 0, 64), v2("q16", 0, 64), one("q4"), A.is_equal)

    for s in range(N):
        if s != rank:
            arrive("c1", 2 * every, codes("landa", 128 * s, 128 * s + 128), plane("landa", 128 * s, 128 * s + 128))
            arrive("n1", every, v2("nl", 8 * s, 8 * s + 8))
    for t in range(4):
        pick("ct", 128 * t, 128 * t + 128, "landa", 512, "offct", t)

    def empty(q, tile, lo, t, bank, n, f):
        o, z = v2(tile, lo + t, lo + 4 * n, 4), v2("ps%d" % bank, 0, n)
        if f == "copy":
            act(o, z, ACT.Copy) if q == "a" else cp(o, z)
        elif f == "relu":
            act(o, z, ACT.Relu, scale=0.0625) if q == "a" else ts(o, z, 0.0, A.max, 0.0625, A.mult)
        else:
            act(o, z, ACT.Copy, scale=0.0625) if q == "a" else ts(o, z, 0.0625, A.mult)

    for t in range(4):
        mm(t, 512, "ct", 128 * t, "wvq", 0)
        empty("avav"[t], "vt", 0, t, t, 512, "copy")
        if t == 1:
            ts(v2("fF", 0, 32), v2("nl", 0, 32), 255.5, A.is_lt)
            cp(v2("nf", 0, 32), v2("nl", 0, 32))
            for m in range(4):
                x = 32 * (m % 2) + 12 + 16 * (m // 2)
                total_of(v2("X", x, x + 1), v2("fF", 8 * m, 8 * m + 8))
            tt(v2("nt", 0, 32), v2("nf", 0, 32), v2("nadd", 0, 32), A.add)
            turn32(v2("ntt", 0, 32), v2("nt", 0, 32))
    dma("s", "ltb", (T.tabrow[0:1, 0:512], v2("tabrow", 0, 512)[1], []), (T.ntt[0:32, 0:16], v2("ntt", 0, 32)[1], []))
    do("g", "partition_broadcast", v2("tab", 0, 520), (T.tabrow[0:1, 0:520], v2("tabrow", 0, 520)[1], []), 128)
    quant("vq", 0, 512, "vt", 0)
    for h, who in enumerate(("aaaa", "aaav")):
        for t in range(4):
            bank = 4 * (1 - h) + t
            mm(bank, 256, "ct", 128 * t, "landa", 256 * h)
            empty(who[t], "at", 1024 * h, t, bank, 256, "relu")
        quant("aq", 256 * h, 256 * h + 256, "at", 1024 * h)
    for lo, n, b0, who in ((0, 256, 4, "aava"), (256, 128, 0, "aaaa"), (384, 128, 4, "avav")):
        for i in range(4):
            mm(b0 + i, n, "vq", 128 * i, "aq", lo)
        if lo == 384:
            for b in (1, 0):
                mm(b, 128, "w2", 144 * b + 16, "hq", 0, True, False)
                mm(b, 128, "w2", 144 * b, "hq", 256, False, True)
            for b in (1, 0):
                mm(2 + b, 128, "w2", 144 * b + 16, "hq", 128, True, False)
        for i in range(4):
            empty(who[i], "ht", 4 * lo, i, b0 + i, n, "scale")
        if lo == 0:
            turn32(v2("xt", 0, 64), v2("X", 0, 64))
            for h in range(2):
                total_of(one("cnt%d" % h), v2("xt", 32 * h, 32 * h + 32))
        quant("hq", lo, lo + n, "ht", 4 * lo)
        if lo == 0:
            for h in range(2):
                ts(half("tb2", h), v2("io2", 0, 128), one("cnt%d" % h), A.is_lt, one("t0a"), A.mult)
    for b in (1, 0):
        mm(2 + b, 128, "w2", 144 * b, "hq", 384, False, True)

    def sign(h):
        act(half("J2", h), half("ind2", h), ACT.Identity, scale=2 * FAR, bias=-FAR)

    gate(2, 0)
    bound(2, 0)
    gate(2, 1)
    member(2, 0)
    sign(0)
    bound(2, 1)
    scan(v2("C2", 0, 128), v2("am", 0, 128), v2("ind2", 0, 128), 0.0, A.mult, A.add)
    member(2, 1)
    sign(1)
    turn32(v2("tC2", 0, 128), v2("C2", 0, 128))
    scan(v2("C2", 128, 416), v2("am", 0, 288), v2("ind2", 128, 416), v2("C2", 127, 128), A.mult, A.add)
    turn32(half("tJ2", 0), half("J2", 0))
    turn32(half("tJ2", 1), half("J2", 1))
    turn32(v2("tC2", 128, 416), v2("C2", 128, 416))
    for h in range(2):
        tt(v2("D2", 32 * h, 32 * h + 32), v2("tC2", 128 * h, 128 * h + 128, 4), v2("tC2", 272, 400, 4), A.add)
    tt(v2("M2", 0, 64), v2("D2", 0, 64), v2("tJ2", 0, 256, 4), A.min)
    scan(v2("R2", 0, 64), v2("a2", 0, 64), v2("M2", 0, 64), 0.0, A.add, A.max)
    tt(v2("dst2", 0, 16), v2("R2", 3, 64, 4), v2("dmp", 0, 16), A.max)
    ts(v2("do2", 0, 16), v2("dst2", 0, 16), 4.0, A.mult, 256.0, A.add)
    cp(by(v2("win2", 0, 2320), v2("do2", 0, 16)), v2("val2", 0, 256))
    spread("win2", LIST2, "wd2")
    for hf in range(2):
        a, b = 16 * hf, 16 * hf + 16
        turn32(v3("t22", a, b, 0, 32), v3("wd2", a, b, 0, 32))
        tt(v2("l2", a, b), v3i("t22", a, b, 0), v3i("t22", a, b, 16), A.add)
        cp(v2("off2", a, b), v2("l2", a, b))
        if hf == 0:
            pick("slotb", 0, 256, "hq", 640, "off2", 0)
        else:
            tt(v2("pd", 0, 32), v2("l2", 0, 32), v2("dm1", 0, 32), A.mult)
            pick("slotb", 256, 384, "hq", 640, "off2", 2)
        send_cols(far_ks if hf == 0 else near_ks, "c2_%d" % rank, "s2_%d" % rank, "slotb", "landb")
    scan(v2("pds", 0, 32), v2("f8", 0, 32), v2("pd", 0, 32), 0.0, A.mult, A.add)
    cp(v2("offD", 0, 4), v2("pds", 7, 32, 8))
    tt(v2("gm", 0, 64), by(v2("tab", 0, 520), v2("offD", 0, 4)), v2("dm2", 0, 64), A.mult)
    scan(v2("gms", 0, 64), v2("f16", 0, 64), v2("gm", 0, 64), 0.0, A.mult, A.add)
    cp(v2("idu", 0, 4), v2("gms", 15, 64, 16))
    send(all_ks, "n2", [(v2("idu", k, k + 1), v2("idl", 8 * rank, 8 * rank + 1)) for k in all_ks])
    pick("landb", 128 * rank, 128 * rank + 128, "hq", 640, "off2", 3)
    cp(v2("idl", 8 * rank, 8 * rank + 1), v2("idu", 3, 4))
    quant("wq", 0, 128, "wb", 0)

    for s in range(N):
        if s != rank:
            arrive("c2_%d" % s, share[s], codes("landb", 128 * s, 128 * s + 128))
            arrive("s2_%d" % s, share[s], plane("landb", 128 * s, 128 * s + 128))
            arrive("n2", every, v2("idl", 8 * s, 8 * s + 1))
    turn = [rank] + near + off

    def store_codes(q, s):
        dma(q, "oc%d" % s, ext(T.oc[:, 512 * s:512 * s + 512]), codes("landb", 128 * s, 128 * s + 128, dt.uint8))

    for s in [rank] + off:
        store_codes("s", s)
    for i, s in enumerate(turn):
        if s in near:
            store_codes("a", s)
        bank = (6, 7, 2, 3)[i]
        mm(bank, 128, "wq", 0, "landb", 128 * s)
        o, z = v2("yb", 128 * s, 128 * s + 128), v2("ps%d" % bank, 0, 128)
        if i < 3:
            act(o, z, ACT.Copy)
        else:
            cp(o, z)
        dma("a" if i < 3 else "s", "yy%d" % s, ext(T.y[:, 128 * s:128 * s + 128]), o)
    for k in range(4):
        dma("a" if k % 2 else "s", "os%d" % k, ext(T.osc[4 * k:4 * k + 4, :]),
            (T.landbs[32 * k:32 * k + 4, 0:512], plane("landb", 0, 512)[1], []))
    ts(v2("idp", 0, 4), v2("idl", 0, 32, 8), -1.0, A.add)
    turn32(v2("idt", 0, 32), v2("idp", 0, 32))
    for s in range(N):
        dma("a" if s % 2 else "s", "ii%d" % s, ext(T["id"][0:1, 128 * s:128 * s + 128]),
            (T.idt[s:128:32, 0:32], v2("idt", 0, 32)[1], []))
    total["sent"] = sent[0]
    for sem in SEMAPHORES:
        if total.get(sem, 0) > waited.get(sem, 0):
            g.wait_ge(T.sem[sem], total[sem])
